import numpy as np, ml_dtypes
CORES = [25,29,65,69,153,157,193,197]
N = 8
import mx_ref
BF = ml_dtypes.bfloat16
def gentries(a):
    return np.ascontiguousarray(a.reshape(8, 16, -1).transpose(0, 2, 1)).reshape(8, -1)
def gtable(e):
    e = np.asarray(e); return np.ascontiguousarray(e.reshape(8, -1, 16).transpose(0, 2, 1)).reshape(128, -1).astype(np.int32)
def gcols(t, e):
    v = np.concatenate([t.reshape(8, 16, -1, 4), np.zeros((8, 16, 1, 4), BF)], axis=2)
    return np.ascontiguousarray(np.stack([v[g][:, e[g]] for g in range(8)])).reshape(128, -1)
def tile(rs):
    return np.stack(rs, axis=2).reshape(128, -1).astype(BF)
def cut(t, i, w=512):
    return t[:, w * i:w * i + w]
def pick(q, e):
    c = np.concatenate([q[0].reshape(128, -1, 4), np.zeros((128, 1, 4), np.uint8)], axis=1); s = np.concatenate([q[1], np.ones((16, 1), np.uint8)], axis=1)
    return (np.ascontiguousarray(c[:, e].reshape(128, -1)), np.ascontiguousarray(s[:, e]))
def join(*qs):
    return (np.concatenate([q[0] for q in qs], axis=1), np.concatenate([q[1] for q in qs], axis=1))
def put(q, e, v):
    c, s = q[0].reshape(128, -1, 4).copy(), q[1].copy(); c[:, e] = v[0].reshape(128, -1, 4); s[:, e] = v[1]
    return (c.reshape(128, -1), s)
def pk(c, s):
    return (np.ascontiguousarray(c), mx_ref.live(s))
def emit(q):
    return q[0], q[1]
def packed(v, rng):
    q = [mx_ref.quantize(np.ascontiguousarray(v[r])) for r in range(N)]
    return np.stack([a for a, b in q]), np.stack([mx_ref.plane(b, rng) for a, b in q])
def values_of_codes():
    e, c = np.zeros((128, 128, 4), np.float32), np.zeros((128, 2, 4), np.uint8)
    e[np.arange(128), np.arange(128), 0] = 1
    c[:127, :, 0] = np.arange(256).reshape(2, 128).T[:127]
    return mx_ref.matmul(mx_ref.quantize(e.reshape(128, 512).astype(BF)), (c.reshape(128, 8), np.full((16, 2), 127, np.uint8))).T.reshape(-1).astype(np.float64)
CODE_VALUE, SCALE_VALUE = values_of_codes(), 2.0 ** (np.arange(256) - 127.0)
def decode(q):
    return (CODE_VALUE[q[0]].reshape(16, 8, -1, 4) * SCALE_VALUE[q[1]][:, None, :, None] + 0.0).reshape(128, -1).astype(np.float32)
def f(rng, *shape):
    return mx_ref.flush((rng.standard_normal(shape, dtype=np.float32) * np.exp2(rng.integers(-2, 3, shape[:-1] + (1,)))).astype(BF))
def wide(rng, *shape, cols=0):
    v = rng.standard_normal(shape, dtype=np.float32) * np.exp2(rng.integers(-12, 13, shape)).astype(np.float32)
    if cols: v *= np.repeat(np.exp2(rng.integers(-cols, cols + 1, shape[:-2] + (1, shape[-1] // 4))) * (rng.random(shape[:-2] + (1, shape[-1] // 4)) > 0.0625), 4, axis=-1).astype(np.float32)
    return mx_ref.flush(v.astype(BF))
C, S = 192, 32
def stored(j):
    e = j.reshape(2, 8, N, C).transpose(2, 1, 0, 3).reshape(N, 8, 2 * C)
    return np.stack([gtable(e[r]) for r in range(N)])
def both(a):
    return np.stack([gentries(a[r]) for r in range(N)]).reshape(N, 8, 2, C).transpose(2, 1, 0, 3).reshape(2, 8, N * C)
def seats(rng):
    p = rng.permutation(N)
    return p, [np.stack([rng.permutation(C) for r in range(N)]) for h in range(3)]
def place(rng, s, u, seat=None, bits=False):
    p, w = seat or seats(rng)
    n = []
    for h, o in zip((np.zeros(C, int), np.array(s), np.array(u)), w):
        b = p[np.arange(N)[:, None] ^ h if bits else (np.arange(N)[:, None] + h) % N]
        n.append(C * b + o[b, np.arange(C)])
    j, k = np.zeros(N * C, int), np.zeros(N * C, int)
    j[n[0]], k[n[0]] = n[1], n[2]
    return j, k
def roam(rng):
    s, u = [0] * C, [0] * C
    n = [[0] * N for k in range(3)]
    n[0][0] = n[1][0] = n[2][0] = C
    def add(a, b, w):
        n[0][a] += w
        n[1][b] += w
        n[2][(b - a) % N] += w
    for t, a, b in zip(rng.integers(0, C, 6 * C).tolist(), rng.integers(0, N, 6 * C).tolist(), rng.integers(0, N, 6 * C).tolist()):
        add(s[t], u[t], -1)
        add(a, b, 1)
        if max(max(m[1:]) for m in n) <= S:
            s[t], u[t] = a, b
        else:
            add(a, b, -1)
            add(s[t], u[t], 1)
    return s, u
def brim(rng, kind):
    s = np.zeros(C, int)
    m = np.repeat(1 + rng.permutation(N - 1), S)[:C]
    s[:len(m)] = m
    z = np.zeros(C, int)
    return ((s, s), (s, z), (z, s), (z, z))[kind]
def apart(n):
    x = np.array({4: [1, 2, 3], 8: [1, 2, 4, 3, 6, 7, 5]}[N])
    t = np.arange(C)
    return [np.where(t < 192, x[(t + h) % (N - 1)], 0) for h in ((0, 1), (3, 2))[n]]
def lists_of(rng, steps):
    e = [[place(rng, *steps[n][g]) for g in range(8)] for n in range(2)]
    return np.array([[p[0] for p in h] for h in e]), np.array([[p[1] for p in h] for h in e])
def big(v, k, low=-12):
    v = v.astype(np.float32) * np.float32(k)
    v[np.abs(v) < np.float32(2.0 ** low)] = 0
    return v.astype(BF)
def weights(rng, k, low=-20):
    c, p = packed(big(f(rng, N, 128, 2048), k, low), rng)
    return {"wc": c, "ws": p}
def numbers_of(rng):
    return {"xb": big(f(rng, N, 128, 4 * C), 1), "xc": big(f(rng, N, 128, 4 * C), 1), "v": np.array(f(rng, N, 128, 512))}
def with_lists(d, jk):
    return {**d, "jb": stored(jk[0]), "kc": stored(jk[1])}
def setup_inputs(rng):
    d = {**numbers_of(rng), **weights(rng, 0.25)}
    return with_lists(d, lists_of(rng, [[roam(rng) for g in range(8)] for n in range(2)]))
def setup_inputs_full(rng):
    d = {**numbers_of(rng), **weights(rng, 0.25)}
    return with_lists(d, lists_of(rng, [[brim(rng, k % 4) for k in rng.permutation(8)] for n in range(2)]))
def setup_inputs_shared(rng):
    d = {**numbers_of(rng), **weights(rng, 0.25)}
    s, u = np.zeros(C, int), np.zeros(C, int)
    s[:3 * S] = np.repeat([1, 2, N - 1], S)
    u[:2 * S] = np.repeat([3, 1], S)
    e = []
    for far in rng.permutation(8) % 2:
        p, w = seats(rng)
        if far:
            e.append([place(rng, *apart(n), (p, [np.roll(o, n * 192, axis=1) for o in w]), True) for n in range(2)])
        else:
            e.append([place(rng, s, u, (p, w)), place(rng, s, u, (p, [np.roll(o, 2 * S, axis=1) for o in w]))])
    return with_lists(d, np.array(e).transpose(2, 1, 0, 3))
def setup_inputs_twins(rng):
    d = {**numbers_of(rng), **weights(rng, 0.25)}
    e = [roam(rng) for g in range(8)]
    j, k = lists_of(rng, [e, e])
    g = (rng.permutation(8) % 2 == 0)[:, None]
    j[1], k[1] = np.where(g, j[0], k[0]), np.where(g, k[0], j[0])
    return with_lists(d, (j, k))
def setup_inputs_gaps(rng):
    d = setup_inputs(rng)
    e = rng.permutation(N)
    d["xb"][e[0]] = 0
    d["xc"][e[1]] = np.tile(d["xc"][e[1]][:, :4], (1, C))
    g = int(rng.integers(8))
    d["xc"][e[2], 16 * g:16 * g + 16] = 0
    return d
def setup_inputs_spread(rng):
    d = {**setup_inputs(rng), **weights(rng, 2.0 ** -8, -24)}
    for n in ("xb", "xc"): d[n] = big(wide(rng, N, 128, 4 * C, cols=3), 2.0 ** -6)
    return d
def check_inputs(d):
    b = []
    for k in ("xb", "xc", "v"):
        a = np.abs(d[k].astype(np.float32))
        if not (np.isfinite(a).all() and ((a == 0) | (a >= 2.0 ** -30) & (a <= 2.0 ** 30)).all()): b.append("a value of " + k)
    e = {k: both(d[k]) for k in ("jb", "kc")}
    for k in ("jb", "kc"):
        if (np.sort(e[k], axis=2) != np.arange(N * C)).any(): b.append("a number that isn't there exactly once in a half and group of " + k)
    if any(((e[k] < 0) | (e[k] >= N * C)).any() for k in e): return b
    own = np.arange(N * C) // C
    over = set()
    for n in range(2):
        for g in range(8):
            j, k = e["jb"][n, g] // C, e["kc"][n, g] // C
            for name, p, q in (("A and B", own, j), ("A and C", own, k), ("B and C", j, k)):
                c = np.bincount(N * p + q, minlength=N * N).reshape(N, N)
                np.fill_diagonal(c, 0)
                if c.max() > S: over.add("too many nonzeros between two ranks: " + name)
    return b + sorted(over)
def held(q):
    return decode(join(*q)).astype(BF)
def pairs(p, q, e, h):
    a, b = [gcols(p, e[n]).astype(np.float32) * gcols(q, h[n]).astype(np.float32) for n in range(2)]
    return (a + b).astype(BF)
def layer(lay, m):
    o = []
    for r in range(N):
        q = mx_ref.quantize(np.ascontiguousarray(cut(m, r, 4 * C)))
        o.append(mx_ref.quantize(tile([mx_ref.matmul(pick(lay[r], np.arange(128 * b, 128 * b + 128)), q) * np.float32(0.03125) for b in range(4)])))
    return o
def reference(xb, xc, v, wc, ws, jb, kc):
    lay = [pk(wc[r], ws[r]) for r in range(N)]
    j, k = both(jb), both(kc)
    oldb = held([mx_ref.quantize(xb[r]) for r in range(N)])
    oldc = held([mx_ref.quantize(xc[r]) for r in range(N)])
    qa = layer(lay, pairs(oldb, oldc, j, k))
    newa = held(qa)
    i = np.argsort(j, axis=2)
    qb = layer(lay, pairs(newa, oldc, i, np.take_along_axis(k, i, axis=2)))
    newb = held(qb)
    i = np.argsort(k, axis=2)
    qc = layer(lay, pairs(newa, newb, i, np.take_along_axis(j, i, axis=2)))
    y = np.zeros((N, 128, 3 * C), np.float32)
    oc, osc = np.zeros((N, 128, 12 * C), np.uint8), np.zeros((N, 16, 3 * C), np.uint8)
    for r in range(N):
        q = join(qa[r], qb[r], qc[r])
        y[r] = mx_ref.matmul(mx_ref.quantize(v[r]), q)
        oc[r], osc[r] = emit(q)
    return {"y": y, "oc": oc, "osc": osc}

@@ -1,0 +1,613 @@
+from concourse.bass import DstId, RemoteDMATransfer
+from concourse.mybir import dt, AluOpType, ActivationFunctionType
+
+NC, C, MARK = 256, 192, 4000.0
+Q4, U8, BF, F32, I32, U16 = "float8_e4m3fn_x4", "uint8", "bfloat16", "float32", "int32", "uint16"
+
+
+def _scratch():
+    s = {}
+
+    def add(names, n, d):
+        for x in names.split():
+            s[x] = ("sbuf", [128, n], d)
+
+    def mx(names, n):
+        for x in names.split():
+            add(x + "q", n, Q4)
+            add(x + "s", n, U8)
+    add("xbt xct nb0 nb1 nb2 m1 m2 m3 nt1 nt2 nt3", 768, BF)
+    add("vt", 512, BF)
+    add("xe xo", 516, BF)
+    add("st1 st2 st3 st4", 1792, BF)
+    add("g1 g2 g3 pr", 1536, BF)
+    mx("ly", 512)
+    mx("vv", 128)
+    mx("e", 1024)
+    mx("co rc mm1 mm2 mm3 nc", 192)
+    mx("ca", 1536)
+    mx("s1 s2 s3 s4", 448)
+    mx("r1 r2 r3 r4", 64)
+    mx("l1 l2 l3 l4", 640)
+    mx("k1 k2 k3 k4 k5 k6", 768)
+    add("jk", 48, I32)
+    add("vr", 384, I32)
+    add("ci", 4, I32)
+    add("ow", 78, I32)
+    add("lam", 78, I32)
+    add("ta tb iy", 28, I32)
+    add("cf", 8, F32)
+    add("ramp", 520, F32)
+    add("ramp2 vi", 448, F32)
+    add("vp vk", 384, F32)
+    add("oh sa", 416, F32)
+    add("rm sb mxx", 208, F32)
+    add("tr xs cn cb w0 w1 w2 iw", 32, F32)
+    add("sw1 sw3 sw4", 2128, F32)
+    add("ts si ti", 896, F32)
+    add("dd", 192, F32)
+    add("zz zt", 128, F32)
+    add("ysb", 576, F32)
+    add("cp cs", 28, U16)
+    add("os", 72, U16)
+    add("og", 112, U16)
+    add("oi", 84, U16)
+    add("od", 384, U16)
+    add("ms1 ms2 ml1 ml2", 56, U16)
+    add("rl1 rl2", 16, U16)
+    s["ps"] = ("psum", [128, 4096], F32)
+    return s
+
+
+SCRATCH = _scratch()
+NPOOL = 120
+SEMAPHORES = (["ls", "rv", "rs", "rg", "acq", "acs", "al1", "al2"] + ["aq%d" % e for e in (1, 2, 3, 4)]
+              + ["as%d" % e for e in (1, 2, 3, 4)] + ["p%d" % i for i in range(NPOOL)])
+
+
+def roads(cores, topo):
+    n = len(cores)
+    others, calls, relay = [], [], {}
+    for a in range(n):
+        ca = cores[a]
+        rest = [b for b in range(n) if b != a]
+        sib = [b for b in rest if cores[b] in topo.cores_of(ca)]
+        far = [b for b in rest if not topo.may_write(ca, cores[b])]
+        near = [b for b in far if topo.host(cores[b]) == topo.host(ca)]
+        others.append(near + [b for b in far if b not in near] + [b for b in rest if b not in sib and b not in far] + sib)
+    for a in range(n):
+        ca, o = cores[a], others[a]
+        oc = [cores[b] for b in o]
+        at = [others[b].index(a) for b in o]
+        home = [c for c in topo.cores_of(ca) if c not in cores and topo.die(c) == topo.die(ca) and topo.may_write(c, oc[0])]
+
+        def beside(d):
+            return [c for c in range(NC) if topo.mates(c, d) and topo.die(c) == topo.die(ca) and topo.may_write(c, d)
+                    and topo.may_write(ca, c)]
+        away = beside(oc[2])
+        off = topo.engines(ca, oc[4])
+        on = [e for e in topo.engines(ca, oc[6]) if e not in off]
+        h = len(off) // 2
+        k = {}
+        own = (C * a, C * a + C)
+        cr = [beside(oc[0])[0], away[1]]
+        k["cs"] = [(home[0], ("cos", 0, C), ("rcs", 0, C), "acs", on[:h]), (home[1], ("cos", 0, C), ("rcs", 0, C), "acs", on[h:]),
+                   (oc[4], ("cos", 0, C), ("cas",) + own, "acs", off[:h]), (oc[5], ("cos", 0, C), ("cas",) + own, "acs", off[h:])]
+        k["cq"] = [(cr[0], ("coq", 0, C), ("rcq", 0, C), "acq", off[:h]), (cr[1], ("coq", 0, C), ("rcq", 0, C), "acq", off[h:]),
+                   (oc[6], ("coq", 0, C), ("caq",) + own, "acq", on)]
+        k["cs2"] = [(oc[6], ("cos", 0, C), ("cas",) + own, "acs", on)]
+        for i in range(2):
+            ee = topo.engines(home[i], oc[2 * i])
+            relay.setdefault(home[i], []).append((0, "acs", [[(oc[2 * i + x], ("rcs", 0, C), ("cas",) + own, "acs", ee[h * x:h * x + h]) for x in range(2)]]))
+            ee = topo.engines(cr[i], oc[2 * i])
+            relay.setdefault(cr[i], []).append((0, "acq", [[(oc[2 * i + x], ("rcq", 0, C), ("caq",) + own, "acq", ee[h * x:h * x + h]) for x in range(2)],
+                                                           [(oc[4 + i], ("rcq", 0, C), ("caq",) + own, "acq", ee)]]))
+        for m, when in ((1, 1), (2, 5)):
+            src, dst, rl, sem = "ms%d" % m, "ml%d" % m, "rl%d" % m, "al%d" % m
+            k["la%d" % m] = [(home[i], (src, 16 * i, 16 * i + 16), (rl, 0, 16), sem, (off, on)[i]) for i in range(2)]
+            k["lb%d" % m] = [(oc[d], (src, 8 * d, 8 * d + 8), (dst, 8 * at[d], 8 * at[d] + 8), sem, (off[:h], off[h:], on)[d - 4]) for d in (4, 5, 6)]
+            for i in range(2):
+                ee = topo.engines(home[i], oc[2 * i])
+                relay[home[i]].append((when, sem, [[(oc[2 * i + x], (rl, 8 * x, 8 * x + 8), (dst, 8 * at[2 * i + x], 8 * at[2 * i + x] + 8), sem, ee[h * x:h * x + h]) for x in range(2)]]))
+        for e, when in ((1, 2), (2, 3), (3, 4), (4, 6)):
+            for y, z in enumerate("qs"):
+                src, dst, rl, sem = "s%d%s" % (e, z), "l%d%s" % (e, z), "r%d%s" % (e, z), "a%s%d" % (z, e)
+                via = home + away
+                k["%sa%d" % (z, e)] = [(via[d], (src, 64 * d, 64 * d + 64), (rl, 0, 64), sem, (on[:h], on[h:], off[:h], off[h:])[d]) for d in range(4)]
+                k["%sb%d" % (z, e)] = [(oc[d], (src, 64 * d, 64 * d + 64), (dst, 64 * at[d], 64 * at[d] + 64), sem, (off[:h], off[h:], on)[d - 4]) for d in (4, 5, 6)]
+                for d in range(4):
+                    relay.setdefault(via[d], []).append((when + 0.5 * y, sem, [[(oc[d], (rl, 0, 64), (dst, 64 * at[d], 64 * at[d] + 64), sem, topo.engines(via[d], oc[d]))]]))
+        calls.append(k)
+    total = {}
+    every = [t for k in calls for c in k.values() for t in c] + [t for st in relay.values() for s in st for c in s[2] for t in c]
+    for t in every:
+        total[(t[0], t[3])] = total.get((t[0], t[3]), 0) + len(t[4])
+    return others, calls, relay, total
+
+
+def view(T, v, wire=False):
+    a = T[v[0]][:, v[1]:v[2]] if len(v) == 3 else T[v[0]][:, v[1]:v[2]:v[3]]
+    return a.bitcast(dt.uint8) if wire and SCRATCH[v[0]][2] == Q4 else a
+
+
+def remote(g, core, T, topo, call):
+    ts = []
+    for d, s, o, sem, ee in call:
+        rid, pid = topo.addr(d, core)
+        ts.append((rid, pid, view(T, s, True), view(T, o, True), T.sem[sem], sum(1 << e for e in ee)))
+    if len(ts) == 1:
+        rid, pid, s, o, sem, m = ts[0]
+        g.remote_dma(o, s, sem, T.sem["ls"], pid, rid, m)
+    else:
+        g.remote_dma_fused([RemoteDMATransfer(dst_ids=[DstId(rid=rid, pnc=pid)], dma_engine_mask=m, remote_sem=sem, src=s, dst=o)
+                            for rid, pid, s, o, sem, m in ts], local_sem=T.sem["ls"])
+    return sum(len(t[4]) for t in call)
+
+
+def clash(a, b):
+    if a[0] != b[0]:
+        return False
+    if a[0] == "ps":
+        return a[1] // 512 <= (b[2] - 1) // 512 and b[1] // 512 <= (a[2] - 1) // 512
+    if a[2] <= b[1] or b[2] <= a[1]:
+        return False
+    return not (len(a) == 4 and len(b) == 4 and a[3] == b[3] and a[1] % a[3] != b[1] % b[3])
+
+
+def emit(g, T, ops):
+    queue = {"g": g, "v": g.vector, "s": g.scalar, "t": g.tensor, "y": g.sync}
+    seen = {}
+    for i, o in enumerate(ops):
+        deps = set()
+        for v, wr in [(x, False) for x in o["r"]] + [(x, True) for x in o["w"]]:
+            for j, u, w2 in seen.get(v[0], []):
+                p = ops[j]
+                if j == i or (p["q"] == "t" and o["q"] == "t") or p["k"] == "r" or o["k"] == "x":
+                    continue
+                if (wr or w2 or (v[0] == "ps" and p["q"] != o["q"])) and clash(v, u):
+                    deps.add(j)
+            seen.setdefault(v[0], []).append((i, v, wr))
+        o["d"] = sorted(deps)
+        for j in deps:
+            ops[j]["n"].add(o["q"])
+    for live in (False, True):
+        known = {q: set() for q in queue}
+        roll = {q: [] for q in "vsg"}
+        pool, count, waited, sent = [], {}, {}, 0
+        used = [set() for o in ops]
+        for i, o in enumerate(ops):
+            q = o["q"]
+            if o["k"] == "x":
+                o["b"] = set()
+                count[o["h"][0]] = o["h"][1]
+                continue
+            for j in reversed(o["d"]):
+                if j in known[q]:
+                    continue
+                used[j].add(q)
+                h = ops[j]["h"]
+                if h == "roll":
+                    h = ("r" + q, len(roll[q]))
+                    known[q].update(roll[q])
+                known[q].add(j)
+                known[q].update(ops[j]["b"])
+                waited[h[0]] = max(waited.get(h[0], 0), h[1])
+                if live:
+                    queue[q].wait_ge(T.sem[h[0]], h[1])
+            o["b"] = set(known[q])
+            ins = o["f"]() if live else None
+            o["h"] = None
+            if o["k"] == "r":
+                sent += ins or 0
+                continue
+            if o["k"] == "c" and o["n"] == {q}:
+                roll[q].append(i)
+                o["h"], s, step = "roll", "r" + q, 1
+                count[s] = len(roll[q])
+            elif o["k"] == "d" or o["n"]:
+                free = [x for x in range(len(pool)) if pool[x] in known[q] and ops[pool[x]]["k"] == o["k"]]
+                if not live or len(pool) < NPOOL // 2 or not free:
+                    pool.append(None)
+                    free = [len(pool) - 1]
+                x = min(free, key=lambda x: pool[x] or 0)
+                pool[x] = i
+                s, step = "p%d" % x, 16 if o["k"] == "d" else 1
+                count[s] = count.get(s, 0) + step
+                o["h"] = (s, count[s])
+            else:
+                continue
+            if live:
+                ins.then_inc(T.sem[s], step)
+        for i, o in enumerate(ops):
+            o["n"] = used[i] | (o["n"] & {o["q"]})
+    g.wait_ge(T.sem["ls"], sent)
+    for s in count:
+        if waited.get(s, 0) < count[s]:
+            g.wait_ge(T.sem[s], count[s])
+
+
+def rank_program(g, core, T, topo):
+    cores = list(T.cores)
+    r = T.rank_of(core)
+    if r is None and not any(core in topo.cores_of(c) or topo.mates(core, c) for c in cores):
+        return
+    others, calls, relay, total = roads(cores, topo)
+    if r is None:
+        sent = 0
+        for when, sem, cs in sorted(relay.get(core, []), key=lambda s: s[0]):
+            g.wait_ge(T.sem[sem], total[(core, sem)])
+            for c in cs:
+                sent += remote(g, core, T, topo, c)
+        if sent:
+            g.wait_ge(T.sem["ls"], sent)
+        return
+    A, AF = AluOpType, ActivationFunctionType
+    ops = []
+    r0 = float(C * r)
+
+    def op(q, k, f, rd, wr, h=None):
+        ops.append({"q": q, "k": k, "f": f, "r": rd, "w": wr, "n": set(), "h": h})
+
+    def ap(v):
+        return view(T, v)
+
+    def col(x):
+        return ap(x) if isinstance(x, tuple) else x
+
+    def ts(o, i, s1, o0, s2=None, o1=None):
+        rd = [i] + [x for x in (s1, s2) if isinstance(x, tuple)]
+        if o1 is None:
+            op("v", "c", lambda: g.vector.tensor_scalar(ap(o), ap(i), col(s1), None, o0), rd, [o])
+        else:
+            op("v", "c", lambda: g.vector.tensor_scalar(ap(o), ap(i), col(s1), col(s2), o0, o1), rd, [o])
+
+    def tt(o, a, b, f):
+        op("v", "c", lambda: g.vector.tensor_tensor(ap(o), ap(a), ap(b), f), [a, b], [o])
+
+    def cp(o, i, q="v"):
+        if q == "v":
+            op("v", "c", lambda: g.vector.tensor_copy(ap(o), ap(i)), [i], [o])
+        else:
+            op("s", "c", lambda: g.scalar.activation(ap(o), ap(i), AF.Copy), [i], [o])
+
+    def ms(o, c):
+        op("v", "c", lambda: g.vector.memset(ap(o), c), [], [o])
+
+    def tr(o, i):
+        op("v", "c", lambda: g.vector.transpose(ap(o), ap(i)), [i], [o])
+
+    def scan(o, a, b, init, o0, o1):
+        op("v", "c", lambda: g.vector.tensor_tensor_scan(ap(o), ap(a), ap(b), col(init), o0, o1),
+           [a, b] + ([init] if isinstance(init, tuple) else []), [o])
+
+    def gather(o, w, f, q="v"):
+        if q == "s":
+            op("s", "c", lambda: g.scalar.activation(ap(o), ap(w).indirect(ap(f)), AF.Copy), [w, f], [o])
+        elif SCRATCH[o[0]][2] == Q4:
+            op("v", "c", lambda: g.vector.tensor_copy(ap(o).bitcast(dt.uint32), ap(w).bitcast(dt.uint32).indirect(ap(f))), [w, f], [o])
+        else:
+            op("v", "c", lambda: g.vector.tensor_copy(ap(o), ap(w).indirect(ap(f))), [w, f], [o])
+
+    def scatter(w, f, i):
+        op("v", "c", lambda: g.vector.tensor_copy(ap(w).indirect(ap(f)), ap(i)), [i, f], [w])
+
+    def act(o, i, bias, scale):
+        op("s", "c", lambda: g.scalar.activation(ap(o), ap(i), AF.Identity, bias=bias, scale=scale), [i], [o])
+
+    def fill(name, n, c):
+        for x in range(0, n, 448):
+            act((name, x, min(n, x + 448)), ("ramp", 0, min(n, x + 448) - x), c, 0.0)
+
+    def quant(name, lo, hi, i):
+        o, s = (name + "q", lo, hi), (name + "s", lo, hi)
+        op("v", "c", lambda: g.vector.quantize_mx(ap(o), ap(s), ap(i)), [i], [o, s])
+
+    def mm(bank, a, b, start=True, stop=True):
+        vs = [(a[0] + "q",) + a[1:], (a[0] + "s",) + a[1:], (b[0] + "q",) + b[1:], (b[0] + "s",) + b[1:]]
+        o = ("ps", 512 * bank, 512 * bank + b[2] - b[1])
+        op("t", "c", lambda: g.tensor.matmul_mx(ap(o), ap(vs[0]), ap(vs[1]), ap(vs[2]), ap(vs[3]), start, stop), vs, [o])
+
+    def dma(q, o, i, rd, wr):
+        op(q, "d", lambda: (g.sync if q == "y" else g.scalar).dma_start(o, i), rd, wr)
+
+    def send(name):
+        op("g", "r", lambda: remote(g, core, T, topo, calls[r][name]), [t[1] for t in calls[r][name]], [])
+
+    def arrive(sem, *vs):
+        op("x", "x", None, [], list(vs), (sem, total[(core, sem)]))
+
+    def weave(*gens):
+        gens = list(gens)
+        while gens:
+            for x in list(gens):
+                if next(x, "end") == "end":
+                    gens.remove(x)
+
+    cf = [("cf", i, i + 1) for i in range(8)]
+
+    op("g", "c", lambda: g.iota(T.ci[:, 3:4], [[0, 1]], 0, 1), [], [("ci", 3, 4)])
+    op("g", "c", lambda: g.iota(T.ramp[:, 0:520], [[1, 520]], 0, 0, allow_small_or_imprecise_dtypes=True), [], [("ramp", 0, 520)])
+    op("g", "c", lambda: g.iota(T.vr[:, 0:384], [[1, 16], [0, 2], [16, 12]], 448, 0), [], [("vr", 0, 384)])
+    dma("y", T.jk[:, 0:24], T.jb[:], [], [("jk", 0, 24)])
+    dma("s", T.xct[:], T.xc[:], [], [("xct", 0, 768)])
+    dma("y", T.jk[:, 24:48], T.kc[:], [], [("jk", 24, 48)])
+    dma("s", T.xbt[:], T.xb[:], [], [("xbt", 0, 768)])
+    dma("y", T.vr[0:128:16, :], T.jb[:], [], [("vr", 0, 384, 2)])
+    dma("y", T.vr[1:128:16, :], T.kc[:], [], [("vr", 1, 384, 2)])
+    dma("y", T.lyq[:].bitcast(dt.uint8), T.wc[:], [], [("lyq", 0, 512)])
+    dma("y", T.lys[:], T.ws[:], [], [("lys", 0, 512)])
+    dma("y", T.vt[:], T.v[:], [], [("vt", 0, 512)])
+    fill("sw1", 1664, MARK)
+    ms(("ow", 0, 78), -1)
+    ms(("rm", 0, 208), 1.0)
+    ms(("sa", 182, 416), 0.0)
+    ms(("sb", 182, 208), 0.0)
+    ms(("dd", 0, 192), 0.0)
+    ms(("cn", 0, 28), 0.0)
+    for i, m in enumerate((15, 16, 31)):
+        ts(("ci", i, i + 1), ("ci", 3, 4), m, A.bitwise_and)
+    ts(cf[5], ("ci", 3, 4), 4.0, A.mult, 3.0, A.add)
+    ms(("rm", 0, 208, 13), 0.0)
+    ms(("cn", 2, 28, 4), 192.0)
+    ms(("cn", 3, 28, 4), 192.0)
+    cp(("cf", 0, 3), ("ci", 0, 3))
+    ts(cf[6], ("ci", 2, 3), 32.0, A.mult, -1.0, A.add)
+    ts(cf[7], ("ci", 0, 1), 24.0, A.mult)
+    ts(cf[3], ("ci", 1, 2), 0.0625, A.mult)
+    ts(cf[4], ("ci", 1, 2), -0.0625, A.mult, 1.0, A.add)
+    cp(("xs", 0, 1), cf[6])
+    cp(("xs", 16, 17), cf[6])
+    ts(("cp", 0, 24), ("ramp", 0, 24), cf[7], A.add)
+
+    def rank(x, i, extra=()):
+        extra = list(extra)
+        o = 26 * i
+        for n in range(2):
+            ts(("ow", o + 13 * n + 1, o + 13 * n + 13), (x[0], x[1] + 12 * n, x[1] + 12 * n + 12), 1.0 / C, A.mult, 0.5 / C - 0.5, A.add)
+            ts(("sb", 183 + 13 * n, 195 + 13 * n), (x[0], x[1] + 12 * n, x[1] + 12 * n + 12), 448.0 + C * n - r0, A.add)
+        yield
+        for d, b in enumerate(others[r] + [r]):
+            ts(("oh", 26 * d, 26 * d + 26), ("ow", o, o + 26), float(b), A.is_equal)
+        yield
+        scan(("sa", 0, 182), ("rm", 0, 182), ("oh", 0, 182), 0.0, A.mult, A.add)
+        if extra:
+            extra.pop(0)()
+        yield
+        tr(("tr", 0, 32), ("sa", 12, 416, 13))
+        yield
+        for h in (0, 16):
+            scan(("xs", h + 1, h + 16), ("tr", h, h + 15), ("sa", 208, 223), cf[6], A.add, A.add)
+        if extra:
+            extra.pop(0)()
+        yield
+        tr(("oh", 0, 416, 13), ("xs", 0, 32))
+        yield
+        scan(("sb", 0, 182), ("rm", 0, 182), ("oh", 0, 182), 0.0, A.mult, A.add)
+        yield
+        tt(("mxx", 0, 208), ("sb", 0, 208), ("oh", 0, 208), A.mult)
+        yield
+        tt(("mxx", 0, 104), ("mxx", 0, 104), ("mxx", 104, 208), A.add)
+        yield
+        tt(("mxx", 0, 52), ("mxx", 0, 52), ("mxx", 52, 104), A.add)
+        yield
+        tt(("lam", o, o + 26), ("mxx", 0, 26), ("mxx", 26, 52), A.add)
+        yield
+        ts(("ta", 0, 26), ("lam", o, o + 26), 0xFFF0, A.bitwise_and)
+        yield
+        tt(("tb", 0, 26), ("lam", o, o + 26), ("ta", 0, 26), A.add)
+        yield
+        for n in range(2):
+            ts(("os", 24 * i + 12 * n, 24 * i + 12 * n + 12), ("tb", 13 * n + 1, 13 * n + 13), cf[1], A.add)
+        yield
+
+    def unrow(o, row, n):
+        tt(o, ("ts", row, 32 * n, 32), ("ts", row + 16, 32 * n, 32), A.min)
+
+    def slots(sw, i, vals, outs):
+        scatter((sw, 0, 2128), ("os", 24 * i, 24 * i + 24), vals)
+        yield
+        tr(("ts", 0, 896), (sw, 0, 896))
+        yield
+        for x, (row, to, sh) in enumerate(outs):
+            unrow(("w%d" % x, 0, 28), row, 28)
+        yield
+        for x, (row, to, sh) in enumerate(outs):
+            if sh is None:
+                cp(to, ("w%d" % x, 0, 28))
+            else:
+                ts(to, ("w%d" % x, 0, 28), sh, A.add, C - 1.0, A.min)
+        yield
+
+    def invert(sw, i, lst, vals, outs):
+        ts(("iw", 0, 28), lst, 448.0 - r0, A.add)
+        yield
+        tt(("iy", 0, 28), ("iw", 0, 28), ("cn", 0, 28), A.add)
+        yield
+        ts(("ta", 0, 28), ("iy", 0, 28), 0xFFF0, A.bitwise_and)
+        yield
+        tt(("iw", 0, 28), ("iy", 0, 28), ("ta", 0, 28), A.add)
+        yield
+        tt(("iw", 0, 28), ("iw", 0, 28), ("cb", 0, 28), A.min)
+        yield
+        ts(("oi", 28 * i, 28 * i + 28), ("iw", 0, 28), cf[1], A.add)
+        yield
+        scatter((sw, 0, 2128), ("oi", 28 * i, 28 * i + 28), vals)
+        yield
+        tr(("ts", 0, 768), (sw, 896, 1664))
+        yield
+        for row, to in outs:
+            unrow(to, row, 24)
+        yield
+
+    def twice(i):
+        for x in range(2):
+            tr(("zz", 64 * x + 16, 64 * x + 48), ("dd", 64 * i + 32 * x, 64 * i + 32 * x + 32))
+        yield
+        for x in range(2):
+            cp(("zz", 64 * x, 64 * x + 16), ("zz", 64 * x + 16, 64 * x + 32))
+            cp(("zz", 64 * x + 48, 64 * x + 64), ("zz", 64 * x + 32, 64 * x + 48))
+        yield
+        tr(("zt", 0, 128), ("zz", 0, 128))
+        yield
+        cp(("od", 128 * i, 128 * i + 128), ("zt", 0, 128))
+        yield
+
+    def compose(e, nb):
+        st, s = "st%d" % e, "s%d" % e
+        for z, lo, hi in (("a", 0, 256), ("b", 256, 448)):
+            for t in (2, 0, 3, 1):
+                gather((st, 4 * lo + t, 4 * hi, 4), (nb, C * t, C * t + C), ("og", 28 * e - 28 + lo // 16, 28 * e - 28 + hi // 16), "vs"[t // 2])
+            yield
+            quant(s, lo, hi, (st, 4 * lo, 4 * hi))
+            send("q%s%d" % (z, e))
+            send("s%s%d" % (z, e))
+            yield
+
+    def unpack(k, win, n, o, bank):
+        for h in range(2):
+            f = ("od", o + 32 * h, o + 32 * h + 24)
+            gather((k + "s", 384 * h, 384 * h + 384), (win + "s", 0, n), f, "s")
+            gather((k + "q", 384 * h, 384 * h + 384), (win + "q", 0, n), f)
+            for b in range(4):
+                mm(bank + b, ("e", 512 * h + 128 * b, 512 * h + 128 * b + 128), (k, 384 * h, 384 * h + 384), h == 0, h == 1)
+            yield
+
+    def early(k, win, n, o, gt):
+        for x in unpack(k, win, n, o, 4):
+            yield
+        for b in range(4):
+            cp((gt, 384 * b, 384 * b + 384), ("ps", 2048 + 512 * b, 2048 + 512 * b + 384), "s")
+        yield
+
+    def mode(m, e, k, o, outs):
+        arrive("aq%d" % e, ("l%dq" % e, 0, 448))
+        arrive("as%d" % e, ("l%ds" % e, 0, 448))
+        weave(unpack(k, "l%d" % e, 640, o, 0))
+        for b in range(4):
+            tt(("pr", b, 1536, 4), ("ps", 512 * b, 512 * b + 384), ("g%d" % m, 384 * b, 384 * b + 384), A.mult)
+        tt(("m%d" % m, 0, 768), ("pr", 0, 768), ("pr", 768, 1536), A.add)
+        quant("mm%d" % m, 0, C, ("m%d" % m, 0, 768))
+        for b in (2, 0, 3, 1):
+            mm(4 + b, ("ly", 128 * b, 128 * b + 128), ("mm%d" % m, 0, C))
+        for b in (2, 0, 3, 1):
+            i = ("ps", 2048 + 512 * b, 2048 + 512 * b + C)
+            if b < 2:
+                ts(outs[b], i, 0.03125, A.mult)
+            else:
+                act(outs[b], i, 0.0, 0.03125)
+
+    def keep(nb, nt, lands):
+        for t in range(4):
+            cp((nt, t, 768, 4), (nb, C * t, C * t + C), "s")
+        yield
+        for x in lands:
+            quant(x, 448, 640, (nt, 0, 768))
+        yield
+
+    def store(f, name, lo):
+        dma("y", T.oc[:, 768 * f:768 * f + 768], view(T, (name + "q", lo, lo + C), True), [(name + "q", lo, lo + C)], [])
+        for x in range(4):
+            dma("ys"[x % 2 if f == 2 else 0], T.osc[4 * x:4 * x + 4, C * f:C * f + C], T[name + "s"][32 * x:32 * x + 4, lo:lo + C], [(name + "s", lo, lo + C)], [])
+
+    def product(f, name, lo):
+        mm(f, ("vv", 0, 128), (name, lo, lo + C))
+        cp(("ysb", C * f, C * f + C), ("ps", 512 * f, 512 * f + C), "vs"[f < 2])
+        dma("ys"[f == 2], T.y[:, C * f:C * f + C], T.ysb[:, C * f:C * f + C], [("ysb", C * f, C * f + C)], [])
+
+    def send_c():
+        quant("co", 0, C, ("xct", 0, 768))
+        send("cs")
+        send("cq")
+        send("cs2")
+
+    def consts():
+        for h in range(2):
+            ts(("xe xo".split()[h], 0, 516), ("ramp", 0, 516), cf[5], A.is_equal, cf[4 - h], A.mult)
+            yield
+        for h in range(2):
+            for b in range(4):
+                quant("e", 512 * h + 128 * b, 512 * h + 128 * b + 128, ("xe xo".split()[h], 3 - b, 515 - b))
+                yield
+        quant("ca", C * r, C * r + C, ("xct", 0, 768))
+        yield
+        quant("l1", 448, 640, ("xbt", 0, 768))
+        yield
+        quant("vv", 0, 128, ("vt", 0, 512))
+        yield
+
+    def lists1():
+        unrow(("w2", 0, 28), 2, 28)
+        ts(("cs", 0, 28), ("ramp", 0, 28), 32.0, A.mult, cf[2], A.add)
+        ts(("iw", 0, 28), ("ramp", 0, 28), 16.0, A.mult, cf[0], A.add)
+        cp(("dd", 0, 24), ("jk", 24, 48))
+        ts(("w1", 0, 26), ("lam", 0, 26), 640.0, A.is_ge, float(C), A.mult)
+        yield
+        ts(("og", 28, 56), ("w2", 0, 28), -448.0, A.add, C - 1.0, A.min)
+        ts(("cb", 0, 28), ("iw", 0, 28), 1664.0, A.add)
+        cp(("si", 2, 896, 32), ("iw", 0, 28))
+        cp(("si", 18, 896, 32), ("iw", 0, 28))
+        for n in range(2):
+            tt(("dd", 32 + 12 * n, 44 + 12 * n), ("lam", 13 * n + 1, 13 * n + 13), ("w1", 13 * n + 1, 13 * n + 13), A.subtract)
+        yield
+        for x in twice(0):
+            yield
+
+    def chain(*gens):
+        for x in gens:
+            for y in x:
+                yield
+
+    def rows2():
+        for x in range(2):
+            for h in (0, 16):
+                cp(("si", h + x, 896, 32), ("ml1", x, 56, 2))
+        yield
+        tr(("ti", 0, 896), ("si", 0, 896))
+        gather(("vi", 0, 448), ("ti", 0, 896), ("cs", 0, 28), "s")
+        yield
+
+    weave(rank(("jk", 0), 0, [send_c, lambda: gather(("vp", 0, 384), ("vr", 0, 384), ("cp", 0, 24))]))
+    fill("si", 896, 0.0)
+    for t in range(4):
+        cp(("nb0", C * t, C * t + C), ("xbt", t, 768, 4), "s")
+    fill("sw3", 1664, MARK)
+    weave(slots("sw1", 0, ("vp", 0, 384), [(0, ("ms1", 0, 56, 2), None), (1, ("ms1", 1, 56, 2), None)]))
+    send("la1")
+    send("lb1")
+    weave(lists1(), rank(("jk", 24), 1), consts())
+    arrive("al1", ("ml1", 0, 56))
+    ts(("og", 0, 28), ("ml1", 0, 56, 2), -r0, A.add, C - 1.0, A.min)
+    weave(compose(1, "nb0"))
+    weave(rows2(), invert("sw1", 0, ("ml1", 0, 56, 2), ("vi", 0, 448), [(1, ("dd", 64, 88)), (2, ("dd", 96, 120))]))
+    arrive("acq", ("caq", 0, C * r), ("caq", C * r + C, 1536))
+    arrive("acs", ("cas", 0, C * r), ("cas", C * r + C, 1536))
+    weave(early("k1", "ca", 1536, 0, "g1"), twice(1),
+          slots("sw3", 1, ("vp", 0, 384), [(1, ("ms2", 0, 56, 2), None), (2, ("og", 56, 84), -448.0)]))
+    mode(1, 1, "k2", 64, [("nb1", C * b, C * b + C) for b in range(4)])
+    weave(compose(2, "nb1"))
+    gather(("vk", 0, 384), ("sw1", 896, 1664), ("cs", 0, 24), "s")
+    weave(chain(early("k3", "ca", 1536, 128, "g2"), keep("nb1", "nt1", ("l2", "l3")), compose(3, "nb1")), rank(("dd", 64), 2))
+    fill("sw4", 1664, MARK)
+    act(("ramp2", 0, 448), ("ramp", 0, 448), r0 - 448.0, 1.0)
+    weave(slots("sw4", 2, ("vk", 0, 384), [(1, ("ms2", 1, 56, 2), None), (0, ("og", 84, 112), -r0)]))
+    send("la2")
+    send("lb2")
+    store(0, "l2", 448)
+    mode(2, 2, "k4", 192, [("nb2", C * b, C * b + C) for b in range(4)])
+    weave(compose(4, "nb2"))
+    arrive("al2", ("ml2", 0, 56))
+    weave(invert("sw3", 1, ("ml2", 0, 56, 2), ("ramp", 0, 448), [(2, ("dd", 128, 152))]), keep("nb2", "nt2", ("l4",)))
+    weave(invert("sw4", 2, ("ml2", 1, 56, 2), ("ramp2", 0, 448), [(0, ("w0", 0, 24))]))
+    ts(("dd", 160, 184), ("w0", 0, 24), 448.0 - r0, A.add)
+    product(0, "l2", 448)
+    product(1, "l4", 448)
+    store(1, "l4", 448)
+    weave(twice(2))
+    arrive("aq3", ("l3q", 0, 448))
+    arrive("as3", ("l3s", 0, 448))
+    weave(early("k5", "l3", 640, 256, "g3"))
+    mode(3, 4, "k6", 320, [("nt3", b, 768, 4) for b in range(4)])
+    quant("nc", 0, C, ("nt3", 0, 768))
+    store(2, "nc", 0)
+    product(2, "nc", 0)
+    emit(g, T, ops)

@@ -32,16 +32,16 @@ def _scratch():
     mx("k1 k2 k3 k4 k5 k6", 768)
     add("jk", 48, I32)
     add("vr", 384, I32)
-    add("ci", 4, I32)
+    add("ci", 6, I32)
     add("ow", 78, I32)
     add("lam", 78, I32)
-    add("ta tb iy", 28, I32)
-    add("cf", 8, F32)
+    add("ta tb iy", 52, I32)
+    add("cf", 10, F32)
     add("ramp", 520, F32)
     add("ramp2 vi", 448, F32)
     add("vp vk", 384, F32)
-    add("oh sa", 416, F32)
-    add("rm sb mxx", 208, F32)
+    add("oh sa sb mxx", 416, F32)
+    add("rm", 432, F32)
     add("tr xs cn cb w0 w1 w2 iw", 32, F32)
     add("sw1 sw3 sw4", 2128, F32)
     add("ts si ti", 896, F32)
@@ -61,7 +61,7 @@ def _scratch():
 
 SCRATCH = _scratch()
 NPOOL = 120
-SEMAPHORES = (["ls", "rv", "rs", "rg", "acq", "acs", "al1", "al2"] + ["aq%d" % e for e in (1, 2, 3, 4)]
+SEMAPHORES = (["ls", "rv", "rs", "rg", "acq", "acs", "al1", "al2", "al3"] + ["aq%d" % e for e in (1, 2, 3, 4)]
               + ["as%d" % e for e in (1, 2, 3, 4)] + ["p%d" % i for i in range(NPOOL)])
 
 
@@ -102,13 +102,14 @@ def roads(cores, topo):
             ee = topo.engines(cr[i], oc[2 * i])
             relay.setdefault(cr[i], []).append((0, "acq", [[(oc[2 * i + x], ("rcq", 0, C), ("caq",) + own, "acq", ee[h * x:h * x + h]) for x in range(2)],
                                                            [(oc[4 + i], ("rcq", 0, C), ("caq",) + own, "acq", ee)]]))
-        for m, when in ((1, 1), (2, 5)):
-            src, dst, rl, sem = "ms%d" % m, "ml%d" % m, "rl%d" % m, "al%d" % m
-            k["la%d" % m] = [(home[i], (src, 16 * i, 16 * i + 16), (rl, 0, 16), sem, (off, on)[i]) for i in range(2)]
-            k["lb%d" % m] = [(oc[d], (src, 8 * d, 8 * d + 8), (dst, 8 * at[d], 8 * at[d] + 8), sem, (off[:h], off[h:], on)[d - 4]) for d in (4, 5, 6)]
+        for m, when, x0, w in ((1, 1, 0, 8), (2, 1.5, 0, 4), (3, 3.8, 1, 4)):
+            src, dst, rl, sem = "ms%d" % min(m, 2), "ml%d" % min(m, 2), "rl%d" % min(m, 2), "al%d" % m
+            s0, l0 = 7 * w * x0, 2 * w * x0
+            k["la%d" % m] = [(home[i], (src, s0 + 2 * w * i, s0 + 2 * w * i + 2 * w), (rl, l0, l0 + 2 * w), sem, (off, on)[i]) for i in range(2)]
+            k["lb%d" % m] = [(oc[d], (src, s0 + w * d, s0 + w * d + w), (dst, s0 + w * at[d], s0 + w * at[d] + w), sem, (off[:h], off[h:], on)[d - 4]) for d in (4, 5, 6)]
             for i in range(2):
                 ee = topo.engines(home[i], oc[2 * i])
-                relay[home[i]].append((when, sem, [[(oc[2 * i + x], (rl, 8 * x, 8 * x + 8), (dst, 8 * at[2 * i + x], 8 * at[2 * i + x] + 8), sem, ee[h * x:h * x + h]) for x in range(2)]]))
+                relay[home[i]].append((when, sem, [[(oc[2 * i + x], (rl, l0 + w * x, l0 + w * x + w), (dst, s0 + w * at[2 * i + x], s0 + w * at[2 * i + x] + w), sem, ee[h * x:h * x + h]) for x in range(2)]]))
         for e, when in ((1, 2), (2, 3), (3, 4), (4, 6)):
             for y, z in enumerate("qs"):
                 src, dst, rl, sem = "s%d%s" % (e, z), "l%d%s" % (e, z), "r%d%s" % (e, z), "a%s%d" % (z, e)
@@ -116,7 +117,7 @@ def roads(cores, topo):
                 k["%sa%d" % (z, e)] = [(via[d], (src, 64 * d, 64 * d + 64), (rl, 0, 64), sem, (on[:h], on[h:], off[:h], off[h:])[d]) for d in range(4)]
                 k["%sb%d" % (z, e)] = [(oc[d], (src, 64 * d, 64 * d + 64), (dst, 64 * at[d], 64 * at[d] + 64), sem, (off[:h], off[h:], on)[d - 4]) for d in (4, 5, 6)]
                 for d in range(4):
-                    relay.setdefault(via[d], []).append((when + 0.5 * y, sem, [[(oc[d], (rl, 0, 64), (dst, 64 * at[d], 64 * at[d] + 64), sem, topo.engines(via[d], oc[d]))]]))
+                    relay.setdefault(via[d], []).append((when + 0.05 * y, sem, [[(oc[d], (rl, 0, 64), (dst, 64 * at[d], 64 * at[d] + 64), sem, topo.engines(via[d], oc[d]))]]))
         calls.append(k)
     total = {}
     every = [t for k in calls for c in k.values() for t in c] + [t for st in relay.values() for s in st for c in s[2] for t in c]
@@ -291,8 +292,9 @@ def rank_program(g, core, T, topo):
     def scatter(w, f, i):
         op("v", "c", lambda: g.vector.tensor_copy(ap(w).indirect(ap(f)), ap(i)), [i, f], [w])
 
-    def act(o, i, bias, scale):
-        op("s", "c", lambda: g.scalar.activation(ap(o), ap(i), AF.Identity, bias=bias, scale=scale), [i], [o])
+    def act(o, i, bias, scale, func=AF.Identity):
+        op("s", "c", lambda: g.scalar.activation(ap(o), ap(i), func, bias=col(bias), scale=scale),
+           [i] + ([bias] if isinstance(bias, tuple) else []), [o])
 
     def fill(name, n, c):
         for x in range(0, n, 448):
@@ -323,11 +325,24 @@ def rank_program(g, core, T, topo):
                 if next(x, "end") == "end":
                     gens.remove(x)
 
-    cf = [("cf", i, i + 1) for i in range(8)]
+    def chain(*gens):
+        for x in gens:
+            for y in x:
+                yield
 
-    op("g", "c", lambda: g.iota(T.ci[:, 3:4], [[0, 1]], 0, 1), [], [("ci", 3, 4)])
-    op("g", "c", lambda: g.iota(T.ramp[:, 0:520], [[1, 520]], 0, 0, allow_small_or_imprecise_dtypes=True), [], [("ramp", 0, 520)])
+    def some(x, n):
+        for i in range(n):
+            next(x, None)
+
+    def beside(x, *gens):
+        for y in chain(*gens):
+            next(x, None)
+
+    cf = [("cf", i, i + 1) for i in range(10)]
+
+    op("g", "c", lambda: g.iota(T.ci[:, 5:6], [[0, 1]], 0, 1), [], [("ci", 5, 6)])
     op("g", "c", lambda: g.iota(T.vr[:, 0:384], [[1, 16], [0, 2], [16, 12]], 448, 0), [], [("vr", 0, 384)])
+    op("g", "c", lambda: g.iota(T.ramp[:, 0:520], [[1, 520]], 0, 0, allow_small_or_imprecise_dtypes=True), [], [("ramp", 0, 520)])
     dma("y", T.jk[:, 0:24], T.jb[:], [], [("jk", 0, 24)])
     dma("s", T.xct[:], T.xc[:], [], [("xct", 0, 768)])
     dma("y", T.jk[:, 24:48], T.kc[:], [], [("jk", 24, 48)])
@@ -339,15 +354,16 @@ def rank_program(g, core, T, topo):
     dma("y", T.vt[:], T.v[:], [], [("vt", 0, 512)])
     fill("sw1", 1664, MARK)
     ms(("ow", 0, 78), -1)
-    ms(("rm", 0, 208), 1.0)
-    ms(("sa", 182, 416), 0.0)
-    ms(("sb", 182, 208), 0.0)
+    ms(("rm", 0, 416), 1.0)
+    ms(("rm", 416, 432), 0.0)
+    ms(("sa", 364, 416), 0.0)
+    ms(("sb", 364, 416), 0.0)
     ms(("dd", 0, 192), 0.0)
     ms(("cn", 0, 28), 0.0)
-    for i, m in enumerate((15, 16, 31)):
-        ts(("ci", i, i + 1), ("ci", 3, 4), m, A.bitwise_and)
-    ts(cf[5], ("ci", 3, 4), 4.0, A.mult, 3.0, A.add)
-    ms(("rm", 0, 208, 13), 0.0)
+    for i, m in enumerate((15, 16, 31, 28, 1)):
+        ts(("ci", i, i + 1), ("ci", 5, 6), m, A.bitwise_and)
+    ts(cf[5], ("ci", 5, 6), -4.0, A.mult, -3.0, A.add)
+    ms(("rm", 0, 416, 13), 0.0)
     ms(("cn", 2, 28, 4), 192.0)
     ms(("cn", 3, 28, 4), 192.0)
     cp(("cf", 0, 3), ("ci", 0, 3))
@@ -355,50 +371,54 @@ def rank_program(g, core, T, topo):
     ts(cf[7], ("ci", 0, 1), 24.0, A.mult)
     ts(cf[3], ("ci", 1, 2), 0.0625, A.mult)
     ts(cf[4], ("ci", 1, 2), -0.0625, A.mult, 1.0, A.add)
-    cp(("xs", 0, 1), cf[6])
-    cp(("xs", 16, 17), cf[6])
-    ts(("cp", 0, 24), ("ramp", 0, 24), cf[7], A.add)
+    ts(cf[8], ("ci", 3, 4), 16.0, A.mult, -1.0, A.add)
+    ts(cf[9], ("ci", 4, 5), 32.0, A.mult, cf[8], A.add)
 
-    def rank(x, i, extra=()):
-        extra = list(extra)
-        o = 26 * i
-        for n in range(2):
-            ts(("ow", o + 13 * n + 1, o + 13 * n + 13), (x[0], x[1] + 12 * n, x[1] + 12 * n + 12), 1.0 / C, A.mult, 0.5 / C - 0.5, A.add)
-            ts(("sb", 183 + 13 * n, 195 + 13 * n), (x[0], x[1] + 12 * n, x[1] + 12 * n + 12), 448.0 + C * n - r0, A.add)
-        yield
-        for d, b in enumerate(others[r] + [r]):
-            ts(("oh", 26 * d, 26 * d + 26), ("ow", o, o + 26), float(b), A.is_equal)
-        yield
-        scan(("sa", 0, 182), ("rm", 0, 182), ("oh", 0, 182), 0.0, A.mult, A.add)
-        if extra:
-            extra.pop(0)()
-        yield
-        tr(("tr", 0, 32), ("sa", 12, 416, 13))
-        yield
-        for h in (0, 16):
-            scan(("xs", h + 1, h + 16), ("tr", h, h + 15), ("sa", 208, 223), cf[6], A.add, A.add)
-        if extra:
-            extra.pop(0)()
-        yield
-        tr(("oh", 0, 416, 13), ("xs", 0, 32))
-        yield
-        scan(("sb", 0, 182), ("rm", 0, 182), ("oh", 0, 182), 0.0, A.mult, A.add)
-        yield
-        tt(("mxx", 0, 208), ("sb", 0, 208), ("oh", 0, 208), A.mult)
-        yield
-        tt(("mxx", 0, 104), ("mxx", 0, 104), ("mxx", 104, 208), A.add)
-        yield
-        tt(("mxx", 0, 52), ("mxx", 0, 52), ("mxx", 52, 104), A.add)
-        yield
-        tt(("lam", o, o + 26), ("mxx", 0, 26), ("mxx", 26, 52), A.add)
-        yield
-        ts(("ta", 0, 26), ("lam", o, o + 26), 0xFFF0, A.bitwise_and)
-        yield
-        tt(("tb", 0, 26), ("lam", o, o + 26), ("ta", 0, 26), A.add)
-        yield
-        for n in range(2):
-            ts(("os", 24 * i + 12 * n, 24 * i + 12 * n + 12), ("tb", 13 * n + 1, 13 * n + 13), cf[1], A.add)
-        yield
+    def rank(x, i, nt, base, extra=None):
+        extra = extra or {}
+        o, w = 26 * i, 26 * nt
+
+        def steps():
+            for n in range(2 * nt):
+                ts(("ow", o + 13 * n + 1, o + 13 * n + 13), (x[0], x[1] + 12 * n, x[1] + 12 * n + 12), 1.0 / C, A.mult, 0.5 / C - 0.5, A.add)
+            cp(("xs", 0, 1), base)
+            cp(("xs", 16, 17), base)
+            yield
+            for d, b in enumerate(others[r] + [r]):
+                ts(("oh", w * d, w * d + w), ("ow", o, o + w), float(b), A.is_equal)
+            yield
+            scan(("sa", 0, 7 * w), ("rm", 0, 7 * w), ("oh", 0, 7 * w), 0.0, A.mult, A.add)
+            for n in range(2 * nt):
+                ts(("sb", 7 * w + 13 * n + 1, 7 * w + 13 * n + 13), (x[0], x[1] + 12 * n, x[1] + 12 * n + 12), 448.0 + C * (n % 2) - r0, A.add)
+            yield
+            tr(("tr", 0, 32), ("sa", 12, 416, 13))
+            yield
+            for h in (0, 16):
+                scan(("xs", h + 1, h + 16), ("tr", h, h + 15), ("rm", 416, 431), base, A.add, A.add)
+            yield
+            tr(("oh", 0, 416, 13), ("xs", 0, 32))
+            yield
+            scan(("sb", 0, 7 * w), ("rm", 0, 7 * w), ("oh", 0, 7 * w), 0.0, A.mult, A.add)
+            yield
+            tt(("mxx", 0, 8 * w), ("sb", 0, 8 * w), ("oh", 0, 8 * w), A.mult)
+            yield
+            tt(("mxx", 0, 4 * w), ("mxx", 0, 4 * w), ("mxx", 4 * w, 8 * w), A.add)
+            yield
+            tt(("mxx", 0, 2 * w), ("mxx", 0, 2 * w), ("mxx", 2 * w, 4 * w), A.add)
+            yield
+            tt(("lam", o, o + w), ("mxx", 0, w), ("mxx", w, 2 * w), A.add)
+            yield
+            ts(("ta", 0, w), ("lam", o, o + w), 0xFFF0, A.bitwise_and)
+            yield
+            tt(("tb", 0, w), ("lam", o, o + w), ("ta", 0, w), A.add)
+            yield
+            for n in range(2 * nt):
+                ts(("os", 24 * i + 12 * n, 24 * i + 12 * n + 12), ("tb", 13 * n + 1, 13 * n + 13), cf[1], A.add)
+            yield
+        for n, y in enumerate(steps()):
+            if n in extra:
+                extra[n]()
+            yield
 
     def unrow(o, row, n):
         tt(o, ("ts", row, 32 * n, 32), ("ts", row + 16, 32 * n, 32), A.min)
@@ -439,24 +459,25 @@ def rank_program(g, core, T, topo):
             unrow(to, row, 24)
         yield
 
-    def twice(i):
-        for x in range(2):
+    def twice(i, xs=(0, 1)):
+        for x in xs:
             tr(("zz", 64 * x + 16, 64 * x + 48), ("dd", 64 * i + 32 * x, 64 * i + 32 * x + 32))
         yield
-        for x in range(2):
+        for x in xs:
             cp(("zz", 64 * x, 64 * x + 16), ("zz", 64 * x + 16, 64 * x + 32))
             cp(("zz", 64 * x + 48, 64 * x + 64), ("zz", 64 * x + 32, 64 * x + 48))
         yield
-        tr(("zt", 0, 128), ("zz", 0, 128))
+        lo, hi = 64 * xs[0], 64 * xs[-1] + 64
+        tr(("zt", lo, hi), ("zz", lo, hi))
         yield
-        cp(("od", 128 * i, 128 * i + 128), ("zt", 0, 128))
+        cp(("od", 128 * i + lo, 128 * i + hi), ("zt", lo, hi))
         yield
 
-    def compose(e, nb):
+    def compose(e, nb, qs="vvss", parts=(("a", 0, 256), ("b", 256, 448))):
         st, s = "st%d" % e, "s%d" % e
-        for z, lo, hi in (("a", 0, 256), ("b", 256, 448)):
+        for z, lo, hi in parts:
             for t in (2, 0, 3, 1):
-                gather((st, 4 * lo + t, 4 * hi, 4), (nb, C * t, C * t + C), ("og", 28 * e - 28 + lo // 16, 28 * e - 28 + hi // 16), "vs"[t // 2])
+                gather((st, 4 * lo + t, 4 * hi, 4), (nb, C * t, C * t + C), ("og", 28 * e - 28 + lo // 16, 28 * e - 28 + hi // 16), qs[t])
             yield
             quant(s, lo, hi, (st, 4 * lo, 4 * hi))
             send("q%s%d" % (z, e))
@@ -468,8 +489,8 @@ def rank_program(g, core, T, topo):
             f = ("od", o + 32 * h, o + 32 * h + 24)
             gather((k + "s", 384 * h, 384 * h + 384), (win + "s", 0, n), f, "s")
             gather((k + "q", 384 * h, 384 * h + 384), (win + "q", 0, n), f)
-            for b in range(4):
-                mm(bank + b, ("e", 512 * h + 128 * b, 512 * h + 128 * b + 128), (k, 384 * h, 384 * h + 384), h == 0, h == 1)
+            for hh, b in (((0, 0), (0, 1)), ((1, 0), (0, 2), (1, 1), (0, 3), (1, 2), (1, 3)))[h]:
+                mm(bank + b, ("e", 512 * hh + 128 * b, 512 * hh + 128 * b + 128), (k, 384 * hh, 384 * hh + 384), hh == 0, hh == 1)
             yield
 
     def early(k, win, n, o, gt):
@@ -479,14 +500,16 @@ def rank_program(g, core, T, topo):
             cp((gt, 384 * b, 384 * b + 384), ("ps", 2048 + 512 * b, 2048 + 512 * b + 384), "s")
         yield
 
-    def mode(m, e, k, o, outs):
+    def mode(m, e, k, o, outs, fl):
         arrive("aq%d" % e, ("l%dq" % e, 0, 448))
         arrive("as%d" % e, ("l%ds" % e, 0, 448))
         weave(unpack(k, "l%d" % e, 640, o, 0))
+        some(fl, 2)
         for b in range(4):
             tt(("pr", b, 1536, 4), ("ps", 512 * b, 512 * b + 384), ("g%d" % m, 384 * b, 384 * b + 384), A.mult)
         tt(("m%d" % m, 0, 768), ("pr", 0, 768), ("pr", 768, 1536), A.add)
         quant("mm%d" % m, 0, C, ("m%d" % m, 0, 768))
+        some(fl, 2)
         for b in (2, 0, 3, 1):
             mm(4 + b, ("ly", 128 * b, 128 * b + 128), ("mm%d" % m, 0, C))
         for b in (2, 0, 3, 1):
@@ -520,10 +543,10 @@ def rank_program(g, core, T, topo):
         send("cq")
         send("cs2")
 
+    def rows1():
+        ts(("cp", 0, 24), ("ramp", 0, 24), cf[7], A.add)
+
     def consts():
-        for h in range(2):
-            ts(("xe xo".split()[h], 0, 516), ("ramp", 0, 516), cf[5], A.is_equal, cf[4 - h], A.mult)
-            yield
         for h in range(2):
             for b in range(4):
                 quant("e", 512 * h + 128 * b, 512 * h + 128 * b + 128, ("xe xo".split()[h], 3 - b, 515 - b))
@@ -540,22 +563,17 @@ def rank_program(g, core, T, topo):
         ts(("cs", 0, 28), ("ramp", 0, 28), 32.0, A.mult, cf[2], A.add)
         ts(("iw", 0, 28), ("ramp", 0, 28), 16.0, A.mult, cf[0], A.add)
         cp(("dd", 0, 24), ("jk", 24, 48))
-        ts(("w1", 0, 26), ("lam", 0, 26), 640.0, A.is_ge, float(C), A.mult)
+        ts(("tr", 0, 26), ("lam", 0, 26), 640.0, A.is_ge, float(C), A.mult)
         yield
         ts(("og", 28, 56), ("w2", 0, 28), -448.0, A.add, C - 1.0, A.min)
         ts(("cb", 0, 28), ("iw", 0, 28), 1664.0, A.add)
         cp(("si", 2, 896, 32), ("iw", 0, 28))
         cp(("si", 18, 896, 32), ("iw", 0, 28))
         for n in range(2):
-            tt(("dd", 32 + 12 * n, 44 + 12 * n), ("lam", 13 * n + 1, 13 * n + 13), ("w1", 13 * n + 1, 13 * n + 13), A.subtract)
+            tt(("dd", 32 + 12 * n, 44 + 12 * n), ("lam", 13 * n + 1, 13 * n + 13), ("tr", 13 * n + 1, 13 * n + 13), A.subtract)
         yield
         for x in twice(0):
             yield
-
-    def chain(*gens):
-        for x in gens:
-            for y in x:
-                yield
 
     def rows2():
         for x in range(2):
@@ -566,47 +584,64 @@ def rank_program(g, core, T, topo):
         gather(("vi", 0, 448), ("ti", 0, 896), ("cs", 0, 28), "s")
         yield
 
-    weave(rank(("jk", 0), 0, [send_c, lambda: gather(("vp", 0, 384), ("vr", 0, 384), ("cp", 0, 24))]))
+    weave(rank(("jk", 0), 0, 2, cf[9], {1: send_c, 3: rows1, 7: lambda: gather(("vp", 0, 384), ("vr", 0, 384), ("cp", 0, 24))}))
     fill("si", 896, 0.0)
+    fill("sw3", 1664, MARK)
+    act(("xo", 0, 516), ("ramp", 0, 516), cf[5], 1.0, AF.Abs)
+    act(("xe", 0, 516), ("xo", 0, 516), cf[4], -1.0, AF.Relu)
+    act(("xo", 0, 516), ("xo", 0, 516), cf[3], -1.0, AF.Relu)
     for t in range(4):
         cp(("nb0", C * t, C * t + C), ("xbt", t, 768, 4), "s")
-    fill("sw3", 1664, MARK)
+    fill("sw4", 1664, MARK)
+    act(("ramp2", 0, 448), ("ramp", 0, 448), r0 - 448.0, 1.0)
     weave(slots("sw1", 0, ("vp", 0, 384), [(0, ("ms1", 0, 56, 2), None), (1, ("ms1", 1, 56, 2), None)]))
     send("la1")
     send("lb1")
-    weave(lists1(), rank(("jk", 24), 1), consts())
+    x = consts()
+    beside(x, lists1())
+    beside(x, slots("sw3", 1, ("vp", 0, 384), [(1, ("ms2", 0, 28), None), (2, ("og", 56, 84), -448.0)]))
+    send("la2")
+    send("lb2")
+    weave(x)
     arrive("al1", ("ml1", 0, 56))
     ts(("og", 0, 28), ("ml1", 0, 56, 2), -r0, A.add, C - 1.0, A.min)
     weave(compose(1, "nb0"))
     weave(rows2(), invert("sw1", 0, ("ml1", 0, 56, 2), ("vi", 0, 448), [(1, ("dd", 64, 88)), (2, ("dd", 96, 120))]))
     arrive("acq", ("caq", 0, C * r), ("caq", C * r + C, 1536))
     arrive("acs", ("cas", 0, C * r), ("cas", C * r + C, 1536))
-    weave(early("k1", "ca", 1536, 0, "g1"), twice(1),
-          slots("sw3", 1, ("vp", 0, 384), [(1, ("ms2", 0, 56, 2), None), (2, ("og", 56, 84), -448.0)]))
-    mode(1, 1, "k2", 64, [("nb1", C * b, C * b + C) for b in range(4)])
+    x = rank(("dd", 64), 2, 1, cf[6])
+    beside(x, early("k1", "ca", 1536, 0, "g1"), twice(1))
+    mode(1, 1, "k2", 64, [("nb1", C * b, C * b + C) for b in range(4)], x)
     weave(compose(2, "nb1"))
     gather(("vk", 0, 384), ("sw1", 896, 1664), ("cs", 0, 24), "s")
-    weave(chain(early("k3", "ca", 1536, 128, "g2"), keep("nb1", "nt1", ("l2", "l3")), compose(3, "nb1")), rank(("dd", 64), 2))
-    fill("sw4", 1664, MARK)
-    act(("ramp2", 0, 448), ("ramp", 0, 448), r0 - 448.0, 1.0)
-    weave(slots("sw4", 2, ("vk", 0, 384), [(1, ("ms2", 1, 56, 2), None), (0, ("og", 84, 112), -r0)]))
-    send("la2")
-    send("lb2")
+    z = keep("nb1", "nt1", ("l2", "l3"))
+    some(z, 1)
+    weave(early("k3", "ca", 1536, 128, "g2"), x)
+    y = compose(3, "nb1", "ssss", (("a", 0, 448),))
+    weave(z, slots("sw4", 2, ("vk", 0, 384), [(1, ("ms2", 28, 56), None), (0, ("og", 84, 112), -r0)]))
+    send("la3")
+    send("lb3")
+    some(y, 1)
+    arrive("al2", ("ml2", 0, 28))
+    weave(invert("sw3", 1, ("ml2", 0, 28), ("ramp", 0, 448), [(2, ("dd", 128, 152))]))
+    weave(y)
+    send("qb3")
+    send("sb3")
     store(0, "l2", 448)
-    mode(2, 2, "k4", 192, [("nb2", C * b, C * b + C) for b in range(4)])
+    mode(2, 2, "k4", 192, [("nb2", C * b, C * b + C) for b in range(4)], twice(2, (0,)))
     weave(compose(4, "nb2"))
-    arrive("al2", ("ml2", 0, 56))
-    weave(invert("sw3", 1, ("ml2", 0, 56, 2), ("ramp", 0, 448), [(2, ("dd", 128, 152))]), keep("nb2", "nt2", ("l4",)))
-    weave(invert("sw4", 2, ("ml2", 1, 56, 2), ("ramp2", 0, 448), [(0, ("w0", 0, 24))]))
-    ts(("dd", 160, 184), ("w0", 0, 24), 448.0 - r0, A.add)
-    product(0, "l2", 448)
-    product(1, "l4", 448)
-    store(1, "l4", 448)
-    weave(twice(2))
+    arrive("al3", ("ml2", 28, 56))
     arrive("aq3", ("l3q", 0, 448))
     arrive("as3", ("l3s", 0, 448))
-    weave(early("k5", "l3", 640, 256, "g3"))
-    mode(3, 4, "k6", 320, [("nt3", b, 768, 4) for b in range(4)])
+    product(0, "l2", 448)
+    x = invert("sw4", 2, ("ml2", 28, 56), ("ramp2", 0, 448), [(0, ("w0", 0, 24))])
+    beside(x, keep("nb2", "nt2", ("l4",)))
+    product(1, "l4", 448)
+    store(1, "l4", 448)
+    weave(x, early("k5", "l3", 640, 256, "g3"))
+    ts(("dd", 160, 184), ("w0", 0, 24), 448.0 - r0, A.add)
+    weave(twice(2, (1,)))
+    mode(3, 4, "k6", 320, [("nt3", b, 768, 4) for b in range(4)], iter(()))
     quant("nc", 0, C, ("nt3", 0, 768))
     store(2, "nc", 0)
     product(2, "nc", 0)

@@ -344,8 +344,8 @@ def rank_program(g, core, T, topo):
     op("g", "c", lambda: g.iota(T.vr[:, 0:384], [[1, 16], [0, 2], [16, 12]], 448, 0), [], [("vr", 0, 384)])
     op("g", "c", lambda: g.iota(T.ramp[:, 0:520], [[1, 520]], 0, 0, allow_small_or_imprecise_dtypes=True), [], [("ramp", 0, 520)])
     dma("y", T.jk[:, 0:24], T.jb[:], [], [("jk", 0, 24)])
-    dma("s", T.xct[:], T.xc[:], [], [("xct", 0, 768)])
-    dma("y", T.jk[:, 24:48], T.kc[:], [], [("jk", 24, 48)])
+    dma("s", T.jk[:, 24:48], T.kc[:], [], [("jk", 24, 48)])
+    dma("y", T.xct[:], T.xc[:], [], [("xct", 0, 768)])
     dma("s", T.xbt[:], T.xb[:], [], [("xbt", 0, 768)])
     dma("y", T.vr[0:128:16, :], T.jb[:], [], [("vr", 0, 384, 2)])
     dma("y", T.vr[1:128:16, :], T.kc[:], [], [("vr", 1, 384, 2)])
@@ -379,17 +379,17 @@ def rank_program(g, core, T, topo):
         o, w = 26 * i, 26 * nt
 
         def steps():
-            for n in range(2 * nt):
-                ts(("ow", o + 13 * n + 1, o + 13 * n + 13), (x[0], x[1] + 12 * n, x[1] + 12 * n + 12), 1.0 / C, A.mult, 0.5 / C - 0.5, A.add)
             cp(("xs", 0, 1), base)
             cp(("xs", 16, 17), base)
+            for n in range(2 * nt):
+                ts(("ow", o + 13 * n + 1, o + 13 * n + 13), (x[0], x[1] + 12 * n, x[1] + 12 * n + 12), 1.0 / C, A.mult, 0.5 / C - 0.5, A.add)
+            for n in range(2 * nt):
+                ts(("sb", 7 * w + 13 * n + 1, 7 * w + 13 * n + 13), (x[0], x[1] + 12 * n, x[1] + 12 * n + 12), 448.0 + C * (n % 2) - r0, A.add)
             yield
             for d, b in enumerate(others[r] + [r]):
                 ts(("oh", w * d, w * d + w), ("ow", o, o + w), float(b), A.is_equal)
             yield
             scan(("sa", 0, 7 * w), ("rm", 0, 7 * w), ("oh", 0, 7 * w), 0.0, A.mult, A.add)
-            for n in range(2 * nt):
-                ts(("sb", 7 * w + 13 * n + 1, 7 * w + 13 * n + 13), (x[0], x[1] + 12 * n, x[1] + 12 * n + 12), 448.0 + C * (n % 2) - r0, A.add)
             yield
             tr(("tr", 0, 32), ("sa", 12, 416, 13))
             yield
@@ -473,16 +473,23 @@ def rank_program(g, core, T, topo):
         cp(("od", 128 * i + lo, 128 * i + hi), ("zt", lo, hi))
         yield
 
-    def compose(e, nb, qs="vvss", parts=(("a", 0, 256), ("b", 256, 448))):
-        st, s = "st%d" % e, "s%d" % e
-        for z, lo, hi in parts:
-            for t in (2, 0, 3, 1):
-                gather((st, 4 * lo + t, 4 * hi, 4), (nb, C * t, C * t + C), ("og", 28 * e - 28 + lo // 16, 28 * e - 28 + hi // 16), qs[t])
-            yield
-            quant(s, lo, hi, (st, 4 * lo, 4 * hi))
-            send("q%s%d" % (z, e))
-            send("s%s%d" % (z, e))
-            yield
+    def compose(e, nb, z, lo, hi, qs):
+        st = "st%d" % e
+        for t in (2, 0, 3, 1):
+            gather((st, 4 * lo + t, 4 * hi, 4), (nb, C * t, C * t + C), ("og", 28 * e - 28 + lo // 16, 28 * e - 28 + hi // 16), qs[t])
+        yield
+        quant("s%d" % e, lo, hi, (st, 4 * lo, 4 * hi))
+        send("q%s%d" % (z, e))
+        send("s%s%d" % (z, e))
+        yield
+
+    def leave(e, nb):
+        x = compose(e, nb, "a", 0, 256, "vvss")
+        some(x, 1)
+        y = compose(e, nb, "b", 256, 448, "ssss")
+        some(y, 1)
+        weave(x)
+        return y
 
     def unpack(k, win, n, o, bank):
         for h in range(2):
@@ -505,9 +512,11 @@ def rank_program(g, core, T, topo):
         arrive("as%d" % e, ("l%ds" % e, 0, 448))
         weave(unpack(k, "l%d" % e, 640, o, 0))
         some(fl, 2)
-        for b in range(4):
-            tt(("pr", b, 1536, 4), ("ps", 512 * b, 512 * b + 384), ("g%d" % m, 384 * b, 384 * b + 384), A.mult)
-        tt(("m%d" % m, 0, 768), ("pr", 0, 768), ("pr", 768, 1536), A.add)
+        for b in range(5):
+            if b < 4:
+                tt(("pr", 384 * b, 384 * b + 384), ("ps", 512 * b, 512 * b + 384), ("g%d" % m, 384 * b, 384 * b + 384), A.mult)
+            if b > 0:
+                tt(("m%d" % m, b - 1, 768, 4), ("pr", 384 * b - 384, 384 * b - C), ("pr", 384 * b - C, 384 * b), A.add)
         quant("mm%d" % m, 0, C, ("m%d" % m, 0, 768))
         some(fl, 2)
         for b in (2, 0, 3, 1):
@@ -530,7 +539,7 @@ def rank_program(g, core, T, topo):
     def store(f, name, lo):
         dma("y", T.oc[:, 768 * f:768 * f + 768], view(T, (name + "q", lo, lo + C), True), [(name + "q", lo, lo + C)], [])
         for x in range(4):
-            dma("ys"[x % 2 if f == 2 else 0], T.osc[4 * x:4 * x + 4, C * f:C * f + C], T[name + "s"][32 * x:32 * x + 4, lo:lo + C], [(name + "s", lo, lo + C)], [])
+            dma("y", T.osc[4 * x:4 * x + 4, C * f:C * f + C], T[name + "s"][32 * x:32 * x + 4, lo:lo + C], [(name + "s", lo, lo + C)], [])
 
     def product(f, name, lo):
         mm(f, ("vv", 0, 128), (name, lo, lo + C))
@@ -584,7 +593,7 @@ def rank_program(g, core, T, topo):
         gather(("vi", 0, 448), ("ti", 0, 896), ("cs", 0, 28), "s")
         yield
 
-    weave(rank(("jk", 0), 0, 2, cf[9], {1: send_c, 3: rows1, 7: lambda: gather(("vp", 0, 384), ("vr", 0, 384), ("cp", 0, 24))}))
+    weave(rank(("jk", 0), 0, 2, cf[9], {1: send_c, 3: rows1, 5: lambda: gather(("vp", 0, 384), ("vr", 0, 384), ("cp", 0, 24))}))
     fill("si", 896, 0.0)
     fill("sw3", 1664, MARK)
     act(("xo", 0, 516), ("ramp", 0, 516), cf[5], 1.0, AF.Abs)
@@ -598,49 +607,64 @@ def rank_program(g, core, T, topo):
     send("la1")
     send("lb1")
     x = consts()
-    beside(x, lists1())
-    beside(x, slots("sw3", 1, ("vp", 0, 384), [(1, ("ms2", 0, 28), None), (2, ("og", 56, 84), -448.0)]))
+    weave(lists1(), slots("sw3", 1, ("vp", 0, 384), [(1, ("ms2", 0, 28), None), (2, ("og", 56, 84), -448.0)]))
     send("la2")
     send("lb2")
     weave(x)
     arrive("al1", ("ml1", 0, 56))
     ts(("og", 0, 28), ("ml1", 0, 56, 2), -r0, A.add, C - 1.0, A.min)
-    weave(compose(1, "nb0"))
-    weave(rows2(), invert("sw1", 0, ("ml1", 0, 56, 2), ("vi", 0, 448), [(1, ("dd", 64, 88)), (2, ("dd", 96, 120))]))
+    y = leave(1, "nb0")
     arrive("acq", ("caq", 0, C * r), ("caq", C * r + C, 1536))
     arrive("acs", ("cas", 0, C * r), ("cas", C * r + C, 1536))
+    x = invert("sw1", 0, ("ml1", 0, 56, 2), ("vi", 0, 448), [(1, ("dd", 64, 88)), (2, ("dd", 96, 120))])
+    beside(x, rows2(), y, early("k1", "ca", 1536, 0, "g1"))
+    weave(x)
     x = rank(("dd", 64), 2, 1, cf[6])
-    beside(x, early("k1", "ca", 1536, 0, "g1"), twice(1))
+    beside(x, twice(1))
+    some(x, 2)
     mode(1, 1, "k2", 64, [("nb1", C * b, C * b + C) for b in range(4)], x)
-    weave(compose(2, "nb1"))
+    y = leave(2, "nb1")
     gather(("vk", 0, 384), ("sw1", 896, 1664), ("cs", 0, 24), "s")
+    weave(x)
+    weave(y)
     z = keep("nb1", "nt1", ("l2", "l3"))
+    x = early("k3", "ca", 1536, 128, "g2")
+    some(x, 2)
     some(z, 1)
-    weave(early("k3", "ca", 1536, 128, "g2"), x)
-    y = compose(3, "nb1", "ssss", (("a", 0, 448),))
-    weave(z, slots("sw4", 2, ("vk", 0, 384), [(1, ("ms2", 28, 56), None), (0, ("og", 84, 112), -r0)]))
-    send("la3")
-    send("lb3")
+    weave(x)
+    y = compose(3, "nb1", "a", 0, 448, "ssss")
     some(y, 1)
     arrive("al2", ("ml2", 0, 28))
-    weave(invert("sw3", 1, ("ml2", 0, 28), ("ramp", 0, 448), [(2, ("dd", 128, 152))]))
+    x = invert("sw3", 1, ("ml2", 0, 28), ("ramp", 0, 448), [(2, ("dd", 128, 152))])
+    beside(x, slots("sw4", 2, ("vk", 0, 384), [(1, ("ms2", 28, 56), None), (0, ("og", 84, 112), -r0)]))
+    send("la3")
+    send("lb3")
+    weave(z, x)
     weave(y)
     send("qb3")
     send("sb3")
     store(0, "l2", 448)
     mode(2, 2, "k4", 192, [("nb2", C * b, C * b + C) for b in range(4)], twice(2, (0,)))
-    weave(compose(4, "nb2"))
+    y = leave(4, "nb2")
     arrive("al3", ("ml2", 28, 56))
     arrive("aq3", ("l3q", 0, 448))
     arrive("as3", ("l3s", 0, 448))
-    product(0, "l2", 448)
     x = invert("sw4", 2, ("ml2", 28, 56), ("ramp2", 0, 448), [(0, ("w0", 0, 24))])
-    beside(x, keep("nb2", "nt2", ("l4",)))
+    some(x, 6)
+    weave(y)
+    z = keep("nb2", "nt2", ("l4",))
+    y = early("k5", "l3", 640, 256, "g3")
+    some(y, 2)
+    some(z, 1)
+    weave(y)
+    some(x, 1)
+    weave(z)
+    product(0, "l2", 448)
     product(1, "l4", 448)
-    store(1, "l4", 448)
-    weave(x, early("k5", "l3", 640, 256, "g3"))
+    weave(x)
     ts(("dd", 160, 184), ("w0", 0, 24), 448.0 - r0, A.add)
     weave(twice(2, (1,)))
+    store(1, "l4", 448)
     mode(3, 4, "k6", 320, [("nt3", b, 768, 4) for b in range(4)], iter(()))
     quant("nc", 0, C, ("nt3", 0, 768))
     store(2, "nc", 0)

from concourse.bass import DstId, RemoteDMATransfer
from concourse.mybir import dt, AluOpType, ActivationFunctionType

NC, C, MARK = 256, 192, 4000.0
Q4, U8, BF, F32, I32, U16 = "float8_e4m3fn_x4", "uint8", "bfloat16", "float32", "int32", "uint16"


def _scratch():
    s = {}

    def add(names, n, d):
        for x in names.split():
            s[x] = ("sbuf", [128, n], d)

    def mx(names, n):
        for x in names.split():
            add(x + "q", n, Q4)
            add(x + "s", n, U8)
    add("xbt xct nb0 nb1 nb2 m1 m2 m3 nt1 nt2 nt3", 768, BF)
    add("vt", 512, BF)
    add("xe xo", 516, BF)
    add("st1 st2 st3 st4", 1792, BF)
    add("g1 g2 g3 pr", 1536, BF)
    mx("ly", 512)
    mx("vv", 128)
    mx("e", 1024)
    mx("co rc mm1 mm2 mm3 nc", 192)
    mx("ca", 1536)
    mx("s1 s2 s3 s4", 448)
    mx("r1 r2 r3 r4", 64)
    mx("l1 l2 l3 l4", 640)
    mx("k1 k2 k3 k4 k5 k6", 768)
    add("jk", 48, I32)
    add("vr", 384, I32)
    add("ci", 6, I32)
    add("ow", 78, I32)
    add("lam", 78, I32)
    add("ta tb iy", 52, I32)
    add("cf", 10, F32)
    add("ramp", 520, F32)
    add("ramp2 vi", 448, F32)
    add("vp vk", 384, F32)
    add("oh sa sb mxx", 416, F32)
    add("rm", 432, F32)
    add("tr xs cn cb w0 w1 w2 iw", 32, F32)
    add("sw1 sw3 sw4", 2128, F32)
    add("ts si ti", 896, F32)
    add("dd", 192, F32)
    add("zz zt", 128, F32)
    add("ysb", 576, F32)
    add("cp cs", 28, U16)
    add("os", 72, U16)
    add("og", 112, U16)
    add("oi", 84, U16)
    add("od", 384, U16)
    add("ms1 ms2 ml1 ml2", 56, U16)
    add("rl1 rl2", 16, U16)
    s["ps"] = ("psum", [128, 4096], F32)
    return s


SCRATCH = _scratch()
NPOOL = 120
SEMAPHORES = (["ls", "rv", "rs", "rg", "acq", "acs", "al1", "al2", "al3"] + ["aq%d" % e for e in (1, 2, 3, 4)]
              + ["as%d" % e for e in (1, 2, 3, 4)] + ["p%d" % i for i in range(NPOOL)])


def roads(cores, topo):
    n = len(cores)
    others, calls, relay = [], [], {}
    for a in range(n):
        ca = cores[a]
        rest = [b for b in range(n) if b != a]
        sib = [b for b in rest if cores[b] in topo.cores_of(ca)]
        far = [b for b in rest if not topo.may_write(ca, cores[b])]
        near = [b for b in far if topo.host(cores[b]) == topo.host(ca)]
        others.append(near + [b for b in far if b not in near] + [b for b in rest if b not in sib and b not in far] + sib)
    for a in range(n):
        ca, o = cores[a], others[a]
        oc = [cores[b] for b in o]
        at = [others[b].index(a) for b in o]
        home = [c for c in topo.cores_of(ca) if c not in cores and topo.die(c) == topo.die(ca) and topo.may_write(c, oc[0])]

        def beside(d):
            return [c for c in range(NC) if topo.mates(c, d) and topo.die(c) == topo.die(ca) and topo.may_write(c, d)
                    and topo.may_write(ca, c)]
        away = beside(oc[2])
        off = topo.engines(ca, oc[4])
        on = [e for e in topo.engines(ca, oc[6]) if e not in off]
        h = len(off) // 2
        k = {}
        own = (C * a, C * a + C)
        cr = [beside(oc[0])[0], away[1]]
        k["cs"] = [(home[0], ("cos", 0, C), ("rcs", 0, C), "acs", on[:h]), (home[1], ("cos", 0, C), ("rcs", 0, C), "acs", on[h:]),
                   (oc[4], ("cos", 0, C), ("cas",) + own, "acs", off[:h]), (oc[5], ("cos", 0, C), ("cas",) + own, "acs", off[h:])]
        k["cq"] = [(cr[0], ("coq", 0, C), ("rcq", 0, C), "acq", off[:h]), (cr[1], ("coq", 0, C), ("rcq", 0, C), "acq", off[h:]),
                   (oc[6], ("coq", 0, C), ("caq",) + own, "acq", on)]
        k["cs2"] = [(oc[6], ("cos", 0, C), ("cas",) + own, "acs", on)]
        for i in range(2):
            ee = topo.engines(home[i], oc[2 * i])
            relay.setdefault(home[i], []).append((0, "acs", [[(oc[2 * i + x], ("rcs", 0, C), ("cas",) + own, "acs", ee[h * x:h * x + h]) for x in range(2)]]))
            ee = topo.engines(cr[i], oc[2 * i])
            relay.setdefault(cr[i], []).append((0, "acq", [[(oc[2 * i + x], ("rcq", 0, C), ("caq",) + own, "acq", ee[h * x:h * x + h]) for x in range(2)],
                                                           [(oc[4 + i], ("rcq", 0, C), ("caq",) + own, "acq", ee)]]))
        for m, when, x0, w in ((1, 1, 0, 8), (2, 1.5, 0, 4), (3, 3.8, 1, 4)):
            src, dst, rl, sem = "ms%d" % min(m, 2), "ml%d" % min(m, 2), "rl%d" % min(m, 2), "al%d" % m
            s0, l0 = 7 * w * x0, 2 * w * x0
            k["la%d" % m] = [(home[i], (src, s0 + 2 * w * i, s0 + 2 * w * i + 2 * w), (rl, l0, l0 + 2 * w), sem, (off, on)[i]) for i in range(2)]
            k["lb%d" % m] = [(oc[d], (src, s0 + w * d, s0 + w * d + w), (dst, s0 + w * at[d], s0 + w * at[d] + w), sem, (off[:h], off[h:], on)[d - 4]) for d in (4, 5, 6)]
            for i in range(2):
                ee = topo.engines(home[i], oc[2 * i])
                relay[home[i]].append((when, sem, [[(oc[2 * i + x], (rl, l0 + w * x, l0 + w * x + w), (dst, s0 + w * at[2 * i + x], s0 + w * at[2 * i + x] + w), sem, ee[h * x:h * x + h]) for x in range(2)]]))
        for e, when in ((1, 2), (2, 3), (3, 4), (4, 6)):
            for y, z in enumerate("qs"):
                src, dst, rl, sem = "s%d%s" % (e, z), "l%d%s" % (e, z), "r%d%s" % (e, z), "a%s%d" % (z, e)
                via = home + away
                k["%sa%d" % (z, e)] = [(via[d], (src, 64 * d, 64 * d + 64), (rl, 0, 64), sem, (on[:h], on[h:], off[:h], off[h:])[d]) for d in range(4)]
                k["%sb%d" % (z, e)] = [(oc[d], (src, 64 * d, 64 * d + 64), (dst, 64 * at[d], 64 * at[d] + 64), sem, (off[:h], off[h:], on)[d - 4]) for d in (4, 5, 6)]
                for d in range(4):
                    relay.setdefault(via[d], []).append((when + 0.05 * y, sem, [[(oc[d], (rl, 0, 64), (dst, 64 * at[d], 64 * at[d] + 64), sem, topo.engines(via[d], oc[d]))]]))
        calls.append(k)
    total = {}
    every = [t for k in calls for c in k.values() for t in c] + [t for st in relay.values() for s in st for c in s[2] for t in c]
    for t in every:
        total[(t[0], t[3])] = total.get((t[0], t[3]), 0) + len(t[4])
    return others, calls, relay, total


def view(T, v, wire=False):
    a = T[v[0]][:, v[1]:v[2]] if len(v) == 3 else T[v[0]][:, v[1]:v[2]:v[3]]
    return a.bitcast(dt.uint8) if wire and SCRATCH[v[0]][2] == Q4 else a


def remote(g, core, T, topo, call):
    ts = []
    for d, s, o, sem, ee in call:
        rid, pid = topo.addr(d, core)
        ts.append((rid, pid, view(T, s, True), view(T, o, True), T.sem[sem], sum(1 << e for e in ee)))
    if len(ts) == 1:
        rid, pid, s, o, sem, m = ts[0]
        g.remote_dma(o, s, sem, T.sem["ls"], pid, rid, m)
    else:
        g.remote_dma_fused([RemoteDMATransfer(dst_ids=[DstId(rid=rid, pnc=pid)], dma_engine_mask=m, remote_sem=sem, src=s, dst=o)
                            for rid, pid, s, o, sem, m in ts], local_sem=T.sem["ls"])
    return sum(len(t[4]) for t in call)


def clash(a, b):
    if a[0] != b[0]:
        return False
    if a[0] == "ps":
        return a[1] // 512 <= (b[2] - 1) // 512 and b[1] // 512 <= (a[2] - 1) // 512
    if a[2] <= b[1] or b[2] <= a[1]:
        return False
    return not (len(a) == 4 and len(b) == 4 and a[3] == b[3] and a[1] % a[3] != b[1] % b[3])


def emit(g, T, ops):
    queue = {"g": g, "v": g.vector, "s": g.scalar, "t": g.tensor, "y": g.sync}
    seen = {}
    for i, o in enumerate(ops):
        deps = set()
        for v, wr in [(x, False) for x in o["r"]] + [(x, True) for x in o["w"]]:
            for j, u, w2 in seen.get(v[0], []):
                p = ops[j]
                if j == i or (p["q"] == "t" and o["q"] == "t") or p["k"] == "r" or o["k"] == "x":
                    continue
                if (wr or w2 or (v[0] == "ps" and p["q"] != o["q"])) and clash(v, u):
                    deps.add(j)
            seen.setdefault(v[0], []).append((i, v, wr))
        o["d"] = sorted(deps)
        for j in deps:
            ops[j]["n"].add(o["q"])
    for live in (False, True):
        known = {q: set() for q in queue}
        roll = {q: [] for q in "vsg"}
        pool, count, waited, sent = [], {}, {}, 0
        used = [set() for o in ops]
        for i, o in enumerate(ops):
            q = o["q"]
            if o["k"] == "x":
                o["b"] = set()
                count[o["h"][0]] = o["h"][1]
                continue
            for j in reversed(o["d"]):
                if j in known[q]:
                    continue
                used[j].add(q)
                h = ops[j]["h"]
                if h == "roll":
                    h = ("r" + q, len(roll[q]))
                    known[q].update(roll[q])
                known[q].add(j)
                known[q].update(ops[j]["b"])
                waited[h[0]] = max(waited.get(h[0], 0), h[1])
                if live:
                    queue[q].wait_ge(T.sem[h[0]], h[1])
            o["b"] = set(known[q])
            ins = o["f"]() if live else None
            o["h"] = None
            if o["k"] == "r":
                sent += ins or 0
                continue
            if o["k"] == "c" and o["n"] == {q}:
                roll[q].append(i)
                o["h"], s, step = "roll", "r" + q, 1
                count[s] = len(roll[q])
            elif o["k"] == "d" or o["n"]:
                free = [x for x in range(len(pool)) if pool[x] in known[q] and ops[pool[x]]["k"] == o["k"]]
                if not live or len(pool) < NPOOL // 2 or not free:
                    pool.append(None)
                    free = [len(pool) - 1]
                x = min(free, key=lambda x: pool[x] or 0)
                pool[x] = i
                s, step = "p%d" % x, 16 if o["k"] == "d" else 1
                count[s] = count.get(s, 0) + step
                o["h"] = (s, count[s])
            else:
                continue
            if live:
                ins.then_inc(T.sem[s], step)
        for i, o in enumerate(ops):
            o["n"] = used[i] | (o["n"] & {o["q"]})
    g.wait_ge(T.sem["ls"], sent)
    for s in count:
        if waited.get(s, 0) < count[s]:
            g.wait_ge(T.sem[s], count[s])


def rank_program(g, core, T, topo):
    cores = list(T.cores)
    r = T.rank_of(core)
    if r is None and not any(core in topo.cores_of(c) or topo.mates(core, c) for c in cores):
        return
    others, calls, relay, total = roads(cores, topo)
    if r is None:
        sent = 0
        for when, sem, cs in sorted(relay.get(core, []), key=lambda s: s[0]):
            g.wait_ge(T.sem[sem], total[(core, sem)])
            for c in cs:
                sent += remote(g, core, T, topo, c)
        if sent:
            g.wait_ge(T.sem["ls"], sent)
        return
    A, AF = AluOpType, ActivationFunctionType
    ops = []
    r0 = float(C * r)

    def op(q, k, f, rd, wr, h=None):
        ops.append({"q": q, "k": k, "f": f, "r": rd, "w": wr, "n": set(), "h": h})

    def ap(v):
        return view(T, v)

    def col(x):
        return ap(x) if isinstance(x, tuple) else x

    def ts(o, i, s1, o0, s2=None, o1=None):
        rd = [i] + [x for x in (s1, s2) if isinstance(x, tuple)]
        if o1 is None:
            op("v", "c", lambda: g.vector.tensor_scalar(ap(o), ap(i), col(s1), None, o0), rd, [o])
        else:
            op("v", "c", lambda: g.vector.tensor_scalar(ap(o), ap(i), col(s1), col(s2), o0, o1), rd, [o])

    def tt(o, a, b, f):
        op("v", "c", lambda: g.vector.tensor_tensor(ap(o), ap(a), ap(b), f), [a, b], [o])

    def cp(o, i, q="v"):
        if q == "v":
            op("v", "c", lambda: g.vector.tensor_copy(ap(o), ap(i)), [i], [o])
        else:
            op("s", "c", lambda: g.scalar.activation(ap(o), ap(i), AF.Copy), [i], [o])

    def ms(o, c):
        op("v", "c", lambda: g.vector.memset(ap(o), c), [], [o])

    def tr(o, i):
        op("v", "c", lambda: g.vector.transpose(ap(o), ap(i)), [i], [o])

    def scan(o, a, b, init, o0, o1):
        op("v", "c", lambda: g.vector.tensor_tensor_scan(ap(o), ap(a), ap(b), col(init), o0, o1),
           [a, b] + ([init] if isinstance(init, tuple) else []), [o])

    def gather(o, w, f, q="v"):
        if q == "s":
            op("s", "c", lambda: g.scalar.activation(ap(o), ap(w).indirect(ap(f)), AF.Copy), [w, f], [o])
        elif SCRATCH[o[0]][2] == Q4:
            op("v", "c", lambda: g.vector.tensor_copy(ap(o).bitcast(dt.uint32), ap(w).bitcast(dt.uint32).indirect(ap(f))), [w, f], [o])
        else:
            op("v", "c", lambda: g.vector.tensor_copy(ap(o), ap(w).indirect(ap(f))), [w, f], [o])

    def scatter(w, f, i):
        op("v", "c", lambda: g.vector.tensor_copy(ap(w).indirect(ap(f)), ap(i)), [i, f], [w])

    def act(o, i, bias, scale, func=AF.Identity):
        op("s", "c", lambda: g.scalar.activation(ap(o), ap(i), func, bias=col(bias), scale=scale),
           [i] + ([bias] if isinstance(bias, tuple) else []), [o])

    def fill(name, n, c):
        for x in range(0, n, 448):
            act((name, x, min(n, x + 448)), ("ramp", 0, min(n, x + 448) - x), c, 0.0)

    def quant(name, lo, hi, i):
        o, s = (name + "q", lo, hi), (name + "s", lo, hi)
        op("v", "c", lambda: g.vector.quantize_mx(ap(o), ap(s), ap(i)), [i], [o, s])

    def mm(bank, a, b, start=True, stop=True):
        vs = [(a[0] + "q",) + a[1:], (a[0] + "s",) + a[1:], (b[0] + "q",) + b[1:], (b[0] + "s",) + b[1:]]
        o = ("ps", 512 * bank, 512 * bank + b[2] - b[1])
        op("t", "c", lambda: g.tensor.matmul_mx(ap(o), ap(vs[0]), ap(vs[1]), ap(vs[2]), ap(vs[3]), start, stop), vs, [o])

    def dma(q, o, i, rd, wr):
        op(q, "d", lambda: (g.sync if q == "y" else g.scalar).dma_start(o, i), rd, wr)

    def send(name):
        op("g", "r", lambda: remote(g, core, T, topo, calls[r][name]), [t[1] for t in calls[r][name]], [])

    def arrive(sem, *vs):
        op("x", "x", None, [], list(vs), (sem, total[(core, sem)]))

    def weave(*gens):
        gens = list(gens)
        while gens:
            for x in list(gens):
                if next(x, "end") == "end":
                    gens.remove(x)

    def chain(*gens):
        for x in gens:
            for y in x:
                yield

    def some(x, n):
        for i in range(n):
            next(x, None)

    def beside(x, *gens):
        for y in chain(*gens):
            next(x, None)

    cf = [("cf", i, i + 1) for i in range(10)]

    op("g", "c", lambda: g.iota(T.ci[:, 5:6], [[0, 1]], 0, 1), [], [("ci", 5, 6)])
    op("g", "c", lambda: g.iota(T.vr[:, 0:384], [[1, 16], [0, 2], [16, 12]], 448, 0), [], [("vr", 0, 384)])
    op("g", "c", lambda: g.iota(T.ramp[:, 0:520], [[1, 520]], 0, 0, allow_small_or_imprecise_dtypes=True), [], [("ramp", 0, 520)])
    dma("y", T.jk[:, 0:24], T.jb[:], [], [("jk", 0, 24)])
    dma("s", T.jk[:, 24:48], T.kc[:], [], [("jk", 24, 48)])
    dma("y", T.xct[:], T.xc[:], [], [("xct", 0, 768)])
    dma("s", T.xbt[:], T.xb[:], [], [("xbt", 0, 768)])
    dma("y", T.vr[0:128:16, :], T.jb[:], [], [("vr", 0, 384, 2)])
    dma("y", T.vr[1:128:16, :], T.kc[:], [], [("vr", 1, 384, 2)])
    dma("y", T.lyq[:].bitcast(dt.uint8), T.wc[:], [], [("lyq", 0, 512)])
    dma("y", T.lys[:], T.ws[:], [], [("lys", 0, 512)])
    dma("y", T.vt[:], T.v[:], [], [("vt", 0, 512)])
    fill("sw1", 1664, MARK)
    ms(("ow", 0, 78), -1)
    ms(("rm", 0, 416), 1.0)
    ms(("rm", 416, 432), 0.0)
    ms(("sa", 364, 416), 0.0)
    ms(("sb", 364, 416), 0.0)
    ms(("dd", 0, 192), 0.0)
    ms(("cn", 0, 28), 0.0)
    for i, m in enumerate((15, 16, 31, 28, 1)):
        ts(("ci", i, i + 1), ("ci", 5, 6), m, A.bitwise_and)
    ts(cf[5], ("ci", 5, 6), -4.0, A.mult, -3.0, A.add)
    ms(("rm", 0, 416, 13), 0.0)
    ms(("cn", 2, 28, 4), 192.0)
    ms(("cn", 3, 28, 4), 192.0)
    cp(("cf", 0, 3), ("ci", 0, 3))
    ts(cf[6], ("ci", 2, 3), 32.0, A.mult, -1.0, A.add)
    ts(cf[7], ("ci", 0, 1), 24.0, A.mult)
    ts(cf[3], ("ci", 1, 2), 0.0625, A.mult)
    ts(cf[4], ("ci", 1, 2), -0.0625, A.mult, 1.0, A.add)
    ts(cf[8], ("ci", 3, 4), 16.0, A.mult, -1.0, A.add)
    ts(cf[9], ("ci", 4, 5), 32.0, A.mult, cf[8], A.add)

    def rank(x, i, nt, base, extra=None):
        extra = extra or {}
        o, w = 26 * i, 26 * nt

        def steps():
            cp(("xs", 0, 1), base)
            cp(("xs", 16, 17), base)
            for n in range(2 * nt):
                ts(("ow", o + 13 * n + 1, o + 13 * n + 13), (x[0], x[1] + 12 * n, x[1] + 12 * n + 12), 1.0 / C, A.mult, 0.5 / C - 0.5, A.add)
            for n in range(2 * nt):
                ts(("sb", 7 * w + 13 * n + 1, 7 * w + 13 * n + 13), (x[0], x[1] + 12 * n, x[1] + 12 * n + 12), 448.0 + C * (n % 2) - r0, A.add)
            yield
            for d, b in enumerate(others[r] + [r]):
                ts(("oh", w * d, w * d + w), ("ow", o, o + w), float(b), A.is_equal)
            yield
            scan(("sa", 0, 7 * w), ("rm", 0, 7 * w), ("oh", 0, 7 * w), 0.0, A.mult, A.add)
            yield
            tr(("tr", 0, 32), ("sa", 12, 416, 13))
            yield
            for h in (0, 16):
                scan(("xs", h + 1, h + 16), ("tr", h, h + 15), ("rm", 416, 431), base, A.add, A.add)
            yield
            tr(("oh", 0, 416, 13), ("xs", 0, 32))
            yield
            scan(("sb", 0, 7 * w), ("rm", 0, 7 * w), ("oh", 0, 7 * w), 0.0, A.mult, A.add)
            yield
            tt(("mxx", 0, 8 * w), ("sb", 0, 8 * w), ("oh", 0, 8 * w), A.mult)
            yield
            tt(("mxx", 0, 4 * w), ("mxx", 0, 4 * w), ("mxx", 4 * w, 8 * w), A.add)
            yield
            tt(("mxx", 0, 2 * w), ("mxx", 0, 2 * w), ("mxx", 2 * w, 4 * w), A.add)
            yield
            tt(("lam", o, o + w), ("mxx", 0, w), ("mxx", w, 2 * w), A.add)
            yield
            ts(("ta", 0, w), ("lam", o, o + w), 0xFFF0, A.bitwise_and)
            yield
            tt(("tb", 0, w), ("lam", o, o + w), ("ta", 0, w), A.add)
            yield
            for n in range(2 * nt):
                ts(("os", 24 * i + 12 * n, 24 * i + 12 * n + 12), ("tb", 13 * n + 1, 13 * n + 13), cf[1], A.add)
            yield
        for n, y in enumerate(steps()):
            if n in extra:
                extra[n]()
            yield

    def unrow(o, row, n):
        tt(o, ("ts", row, 32 * n, 32), ("ts", row + 16, 32 * n, 32), A.min)

    def slots(sw, i, vals, outs):
        scatter((sw, 0, 2128), ("os", 24 * i, 24 * i + 24), vals)
        yield
        tr(("ts", 0, 896), (sw, 0, 896))
        yield
        for x, (row, to, sh) in enumerate(outs):
            unrow(("w%d" % x, 0, 28), row, 28)
        yield
        for x, (row, to, sh) in enumerate(outs):
            if sh is None:
                cp(to, ("w%d" % x, 0, 28))
            else:
                ts(to, ("w%d" % x, 0, 28), sh, A.add, C - 1.0, A.min)
        yield

    def invert(sw, i, lst, vals, outs):
        ts(("iw", 0, 28), lst, 448.0 - r0, A.add)
        yield
        tt(("iy", 0, 28), ("iw", 0, 28), ("cn", 0, 28), A.add)
        yield
        ts(("ta", 0, 28), ("iy", 0, 28), 0xFFF0, A.bitwise_and)
        yield
        tt(("iw", 0, 28), ("iy", 0, 28), ("ta", 0, 28), A.add)
        yield
        tt(("iw", 0, 28), ("iw", 0, 28), ("cb", 0, 28), A.min)
        yield
        ts(("oi", 28 * i, 28 * i + 28), ("iw", 0, 28), cf[1], A.add)
        yield
        scatter((sw, 0, 2128), ("oi", 28 * i, 28 * i + 28), vals)
        yield
        tr(("ts", 0, 768), (sw, 896, 1664))
        yield
        for row, to in outs:
            unrow(to, row, 24)
        yield

    def twice(i, xs=(0, 1)):
        for x in xs:
            tr(("zz", 64 * x + 16, 64 * x + 48), ("dd", 64 * i + 32 * x, 64 * i + 32 * x + 32))
        yield
        for x in xs:
            cp(("zz", 64 * x, 64 * x + 16), ("zz", 64 * x + 16, 64 * x + 32))
            cp(("zz", 64 * x + 48, 64 * x + 64), ("zz", 64 * x + 32, 64 * x + 48))
        yield
        lo, hi = 64 * xs[0], 64 * xs[-1] + 64
        tr(("zt", lo, hi), ("zz", lo, hi))
        yield
        cp(("od", 128 * i + lo, 128 * i + hi), ("zt", lo, hi))
        yield

    def compose(e, nb, z, lo, hi, qs):
        st = "st%d" % e
        for t in (2, 0, 3, 1):
            gather((st, 4 * lo + t, 4 * hi, 4), (nb, C * t, C * t + C), ("og", 28 * e - 28 + lo // 16, 28 * e - 28 + hi // 16), qs[t])
        yield
        quant("s%d" % e, lo, hi, (st, 4 * lo, 4 * hi))
        send("q%s%d" % (z, e))
        send("s%s%d" % (z, e))
        yield

    def leave(e, nb):
        x = compose(e, nb, "a", 0, 256, "vvss")
        some(x, 1)
        y = compose(e, nb, "b", 256, 448, "ssss")
        some(y, 1)
        weave(x)
        return y

    def unpack(k, win, n, o, bank):
        for h in range(2):
            f = ("od", o + 32 * h, o + 32 * h + 24)
            gather((k + "s", 384 * h, 384 * h + 384), (win + "s", 0, n), f, "s")
            gather((k + "q", 384 * h, 384 * h + 384), (win + "q", 0, n), f)
            for hh, b in (((0, 0), (0, 1)), ((1, 0), (0, 2), (1, 1), (0, 3), (1, 2), (1, 3)))[h]:
                mm(bank + b, ("e", 512 * hh + 128 * b, 512 * hh + 128 * b + 128), (k, 384 * hh, 384 * hh + 384), hh == 0, hh == 1)
            yield

    def early(k, win, n, o, gt):
        for x in unpack(k, win, n, o, 4):
            yield
        for b in range(4):
            cp((gt, 384 * b, 384 * b + 384), ("ps", 2048 + 512 * b, 2048 + 512 * b + 384), "s")
        yield

    def mode(m, e, k, o, outs, fl):
        arrive("aq%d" % e, ("l%dq" % e, 0, 448))
        arrive("as%d" % e, ("l%ds" % e, 0, 448))
        weave(unpack(k, "l%d" % e, 640, o, 0))
        some(fl, 2)
        for b in range(5):
            if b < 4:
                tt(("pr", 384 * b, 384 * b + 384), ("ps", 512 * b, 512 * b + 384), ("g%d" % m, 384 * b, 384 * b + 384), A.mult)
            if b > 0:
                tt(("m%d" % m, b - 1, 768, 4), ("pr", 384 * b - 384, 384 * b - C), ("pr", 384 * b - C, 384 * b), A.add)
        quant("mm%d" % m, 0, C, ("m%d" % m, 0, 768))
        some(fl, 2)
        for b in (2, 0, 3, 1):
            mm(4 + b, ("ly", 128 * b, 128 * b + 128), ("mm%d" % m, 0, C))
        for b in (2, 0, 3, 1):
            i = ("ps", 2048 + 512 * b, 2048 + 512 * b + C)
            if b < 2:
                ts(outs[b], i, 0.03125, A.mult)
            else:
                act(outs[b], i, 0.0, 0.03125)

    def keep(nb, nt, lands):
        for t in range(4):
            cp((nt, t, 768, 4), (nb, C * t, C * t + C), "s")
        yield
        for x in lands:
            quant(x, 448, 640, (nt, 0, 768))
        yield

    def store(f, name, lo):
        dma("y", T.oc[:, 768 * f:768 * f + 768], view(T, (name + "q", lo, lo + C), True), [(name + "q", lo, lo + C)], [])
        for x in range(4):
            dma("y", T.osc[4 * x:4 * x + 4, C * f:C * f + C], T[name + "s"][32 * x:32 * x + 4, lo:lo + C], [(name + "s", lo, lo + C)], [])

    def product(f, name, lo):
        mm(f, ("vv", 0, 128), (name, lo, lo + C))
        cp(("ysb", C * f, C * f + C), ("ps", 512 * f, 512 * f + C), "vs"[f < 2])
        dma("ys"[f == 2], T.y[:, C * f:C * f + C], T.ysb[:, C * f:C * f + C], [("ysb", C * f, C * f + C)], [])

    def send_c():
        quant("co", 0, C, ("xct", 0, 768))
        send("cs")
        send("cq")
        send("cs2")

    def rows1():
        ts(("cp", 0, 24), ("ramp", 0, 24), cf[7], A.add)

    def consts():
        for h in range(2):
            for b in range(4):
                quant("e", 512 * h + 128 * b, 512 * h + 128 * b + 128, ("xe xo".split()[h], 3 - b, 515 - b))
                yield
        quant("ca", C * r, C * r + C, ("xct", 0, 768))
        yield
        quant("l1", 448, 640, ("xbt", 0, 768))
        yield
        quant("vv", 0, 128, ("vt", 0, 512))
        yield

    def lists1():
        unrow(("w2", 0, 28), 2, 28)
        ts(("cs", 0, 28), ("ramp", 0, 28), 32.0, A.mult, cf[2], A.add)
        ts(("iw", 0, 28), ("ramp", 0, 28), 16.0, A.mult, cf[0], A.add)
        cp(("dd", 0, 24), ("jk", 24, 48))
        ts(("tr", 0, 26), ("lam", 0, 26), 640.0, A.is_ge, float(C), A.mult)
        yield
        ts(("og", 28, 56), ("w2", 0, 28), -448.0, A.add, C - 1.0, A.min)
        ts(("cb", 0, 28), ("iw", 0, 28), 1664.0, A.add)
        cp(("si", 2, 896, 32), ("iw", 0, 28))
        cp(("si", 18, 896, 32), ("iw", 0, 28))
        for n in range(2):
            tt(("dd", 32 + 12 * n, 44 + 12 * n), ("lam", 13 * n + 1, 13 * n + 13), ("tr", 13 * n + 1, 13 * n + 13), A.subtract)
        yield
        for x in twice(0):
            yield

    def rows2():
        for x in range(2):
            for h in (0, 16):
                cp(("si", h + x, 896, 32), ("ml1", x, 56, 2))
        yield
        tr(("ti", 0, 896), ("si", 0, 896))
        gather(("vi", 0, 448), ("ti", 0, 896), ("cs", 0, 28), "s")
        yield

    weave(rank(("jk", 0), 0, 2, cf[9], {1: send_c, 3: rows1, 5: lambda: gather(("vp", 0, 384), ("vr", 0, 384), ("cp", 0, 24))}))
    fill("si", 896, 0.0)
    fill("sw3", 1664, MARK)
    act(("xo", 0, 516), ("ramp", 0, 516), cf[5], 1.0, AF.Abs)
    act(("xe", 0, 516), ("xo", 0, 516), cf[4], -1.0, AF.Relu)
    act(("xo", 0, 516), ("xo", 0, 516), cf[3], -1.0, AF.Relu)
    for t in range(4):
        cp(("nb0", C * t, C * t + C), ("xbt", t, 768, 4), "s")
    fill("sw4", 1664, MARK)
    act(("ramp2", 0, 448), ("ramp", 0, 448), r0 - 448.0, 1.0)
    weave(slots("sw1", 0, ("vp", 0, 384), [(0, ("ms1", 0, 56, 2), None), (1, ("ms1", 1, 56, 2), None)]))
    send("la1")
    send("lb1")
    x = consts()
    weave(lists1(), slots("sw3", 1, ("vp", 0, 384), [(1, ("ms2", 0, 28), None), (2, ("og", 56, 84), -448.0)]))
    send("la2")
    send("lb2")
    weave(x)
    arrive("al1", ("ml1", 0, 56))
    ts(("og", 0, 28), ("ml1", 0, 56, 2), -r0, A.add, C - 1.0, A.min)
    y = leave(1, "nb0")
    arrive("acq", ("caq", 0, C * r), ("caq", C * r + C, 1536))
    arrive("acs", ("cas", 0, C * r), ("cas", C * r + C, 1536))
    x = invert("sw1", 0, ("ml1", 0, 56, 2), ("vi", 0, 448), [(1, ("dd", 64, 88)), (2, ("dd", 96, 120))])
    beside(x, rows2(), y, early("k1", "ca", 1536, 0, "g1"))
    weave(x)
    x = rank(("dd", 64), 2, 1, cf[6])
    beside(x, twice(1))
    some(x, 2)
    mode(1, 1, "k2", 64, [("nb1", C * b, C * b + C) for b in range(4)], x)
    y = leave(2, "nb1")
    gather(("vk", 0, 384), ("sw1", 896, 1664), ("cs", 0, 24), "s")
    weave(x)
    weave(y)
    z = keep("nb1", "nt1", ("l2", "l3"))
    x = early("k3", "ca", 1536, 128, "g2")
    some(x, 2)
    some(z, 1)
    weave(x)
    y = compose(3, "nb1", "a", 0, 448, "ssss")
    some(y, 1)
    arrive("al2", ("ml2", 0, 28))
    x = invert("sw3", 1, ("ml2", 0, 28), ("ramp", 0, 448), [(2, ("dd", 128, 152))])
    beside(x, slots("sw4", 2, ("vk", 0, 384), [(1, ("ms2", 28, 56), None), (0, ("og", 84, 112), -r0)]))
    send("la3")
    send("lb3")
    weave(z, x)
    weave(y)
    send("qb3")
    send("sb3")
    store(0, "l2", 448)
    mode(2, 2, "k4", 192, [("nb2", C * b, C * b + C) for b in range(4)], twice(2, (0,)))
    y = leave(4, "nb2")
    arrive("al3", ("ml2", 28, 56))
    arrive("aq3", ("l3q", 0, 448))
    arrive("as3", ("l3s", 0, 448))
    x = invert("sw4", 2, ("ml2", 28, 56), ("ramp2", 0, 448), [(0, ("w0", 0, 24))])
    some(x, 6)
    weave(y)
    z = keep("nb2", "nt2", ("l4",))
    y = early("k5", "l3", 640, 256, "g3")
    some(y, 2)
    some(z, 1)
    weave(y)
    some(x, 1)
    weave(z)
    product(0, "l2", 448)
    product(1, "l4", 448)
    weave(x)
    ts(("dd", 160, 184), ("w0", 0, 24), 448.0 - r0, A.add)
    weave(twice(2, (1,)))
    store(1, "l4", 448)
    mode(3, 4, "k6", 320, [("nt3", b, 768, 4) for b in range(4)], iter(()))
    quant("nc", 0, C, ("nt3", 0, 768))
    store(2, "nc", 0)
    product(2, "nc", 0)
    emit(g, T, ops)
